import numpy as np
import ml_dtypes


def mxq(x, axis, fmt="e4m3"):
    dtype, down = {"e4m3": (ml_dtypes.float8_e4m3fn, 7), "e5m2": (ml_dtypes.float8_e5m2, 14)}[fmt]
    v = np.moveaxis(np.asarray(x, np.float32).astype(ml_dtypes.bfloat16).astype(np.float64), axis, -1)
    blocks = v.reshape(v.shape[:-1] + (-1, 32))
    amax = np.abs(blocks).max(-1, keepdims=True)
    byte = np.maximum(np.where(amax > 0, np.frexp(amax)[1] - 1 + 127, 0) - down, 1)
    scale = np.exp2(byte - 127.0)
    codes = (blocks / scale).astype(np.float32).astype(dtype).astype(np.float64)
    return np.moveaxis((codes * scale).reshape(v.shape), -1, axis)


WIDE = False


def mx_kscale(k):
    if not WIDE:
        return np.ones(k)
    levels = np.array([10, -10, 5, -5, 0])
    if k % 512:
        return np.exp2(np.random.permutation(np.resize(levels, k // 32))).repeat(32)
    a = np.empty((k // 512, 16))
    for p in range(k // 512):
        a[p, :8] = np.random.permutation(np.resize(levels, 8))
        for g in range(8):
            far = levels[np.abs(levels - a[p, g]) >= 10]
            a[p, g + 8] = far[np.random.randint(len(far))]
    return np.exp2(a.ravel()).repeat(32)


BF16 = ml_dtypes.bfloat16


def bf(x):
    return np.asarray(x, np.float32).astype(BF16)


def f64(x):
    return np.asarray(x).astype(np.float64)


E2M1 = np.array([0.0, 0.5, 1.0, 1.5, 2.0, 3.0, 4.0, 6.0, -0.0, -0.5, -1.0, -1.5, -2.0, -3.0, -4.0, -6.0])


def pack_weight(w, fmt):
    k, n = w.shape
    w = f64(bf(w)).reshape(k // 32, 32, n)
    amax = np.abs(w).max(1)
    if fmt == "e4m3":
        byte = np.frexp(amax)[1] - 1 + 127 - 7
    else:
        mant, ex = np.frexp(amax / 6.0)
        byte = np.where(mant > 0.5, ex, ex - 1) + 127
    byte = np.clip(np.where(amax > 0, byte, 1), 1, 254)
    scaled = (w * np.exp2(127.0 - byte)[:, None, :]).reshape(k, n).astype(np.float32)
    by_word = np.ascontiguousarray(scaled.reshape(k // 512, 128, 4, n).transpose(0, 1, 3, 2))
    if fmt == "e4m3":
        words = by_word.astype(ml_dtypes.float8_e4m3fn).view(np.uint8)
    else:
        c = by_word.astype(ml_dtypes.float4_e2m1fn).view(np.uint8) & 0xF
        words = c[..., 0::2] | (c[..., 1::2] << 4)
    return np.ascontiguousarray(words), np.ascontiguousarray(byte.astype(np.uint8).reshape(k // 512, 16, n))


def unpack_weight(words, scales, fmt):
    g, p, n, _ = words.shape
    if fmt == "e4m3":
        vals = np.ascontiguousarray(words).view(ml_dtypes.float8_e4m3fn).astype(np.float64)
    else:
        nib = np.empty((g, p, n, 4), np.uint8)
        nib[..., 0::2] = words & 0xF
        nib[..., 1::2] = words >> 4
        vals = E2M1[nib]
    vals = vals * np.repeat(np.exp2(scales.astype(np.float64) - 127.0), 8, axis=1)[..., None]
    return vals.transpose(0, 1, 3, 2).reshape(g * 512, n)
def pack4(w):
    words, scales = pack_weight(w, "e2m1")
    return words.reshape(words.shape[0], 128, -1), scales


def unpack4(words, scales):
    return unpack_weight(words.reshape(words.shape[0], 128, -1, 2), scales, "e2m1")


def planes(Y):
    n, m = Y.shape
    b = f64(bf(Y)).reshape(n // 32, 32, m)
    amax = np.abs(b).max(1)
    byte = np.clip(np.where(amax > 0, np.frexp(amax)[1] - 1 + 127 - 7, 1), 1, 254)
    codes = (b * np.exp2(127.0 - byte)[:, None, :]).reshape(n, m).astype(np.float32).astype(ml_dtypes.float8_e4m3fn).view(np.uint8)
    words = codes.reshape(n // 512, 128, 4, m).transpose(0, 1, 3, 2)
    return np.ascontiguousarray(words), np.ascontiguousarray(byte.astype(np.uint8).reshape(n // 512, 16, m))


N, P, M = 1536, 1024, 1024

PLANT_GAIN = 0.4
MISMATCH = 0.3
SPREAD = 0.8


def setup_inputs():
    s = mx_kscale(N)
    t = mx_kscale(P)
    plant = PLANT_GAIN * np.random.randn(P, N) / np.sqrt(N)
    model = plant + MISMATCH * PLANT_GAIN * np.random.randn(P, N) / np.sqrt(N)
    learn_words, learn_scales = pack4(model / t[:, None] * s[None, :])
    return {
        "u": bf(np.random.randn(N, M) * s[:, None]),
        "r": bf(np.random.randn(P, M) * t[:, None]),
        "plant": bf(plant * t[:, None] / s[None, :]),
        "learn_words": learn_words,
        "learn_scales": learn_scales,
        "w": bf(np.exp(SPREAD * np.random.randn(P, 1)) / t[:, None]),
    }


def reference(u, r, plant, learn_words, learn_scales, w):
    u, r = f64(u), f64(r)
    gq = mxq(f64(plant), 1, "e4m3")
    wl = unpack4(learn_words, learn_scales)
    e = r - (gq @ mxq(u, 0, "e4m3"))
    u1 = u + (wl.T @ mxq(e, 0, "e4m3"))
    y = f64(w) * (r - (gq @ mxq(u1, 0, "e4m3")))
    Y = y
    words, scales = planes(Y)
    return y, words, scales

@@ -1,0 +1,421 @@
+from contextlib import ExitStack
+
+import concourse.mybir as mybir
+from concourse.masks import make_identity
+
+N_IN, N_OUT, TASKS = 1536, 1024, 1024
+FLOPS = 3 * 2 * N_IN * N_OUT * TASKS
+
+F32 = mybir.dt.float32
+BF16 = mybir.dt.bfloat16
+I32 = mybir.dt.int32
+U32 = mybir.dt.uint32
+U8 = mybir.dt.uint8
+FP8X4 = mybir.dt.float8_e4m3fn_x4
+FP4X4 = mybir.dt.float4_e2m1fn_x4
+ALU = mybir.AluOpType
+ACT = mybir.ActivationFunctionType
+
+P = 128
+PACK = 4
+K_PASS = P * PACK
+IN_PASSES = N_IN // K_PASS
+OUT_PASSES = N_OUT // K_PASS
+BANKS = 8
+BANK_COLS = 512
+UNIT = 128
+PAIR = 256
+TURN_BANKS = 4
+G_PARTS = [(0, 2), (2, 1)]
+ORDER = [(2, 0), (2, 1), (1, 2), (1, 3), (3, 0), (2, 2), (1, 4), (2, 3), (1, 5), (2, 4), (3, 1), (1, 6), (2, 5), (1, 7), (2, 6), (3, 2), (2, 7), (3, 3), (3, 4)]
+SCALE_SPANS = [(0, 768), (768, 256)]
+LOAD_SPANS = [(0, 256), (256, 256), (512, 512)]
+LAST_SPANS = [(0, 256), (256, 256), (512, 256), (768, 128), (896, 128)]
+
+
+def tile_lifted_learning_control_error_k1_kernel(tc, u, r, plant, learn_words, learn_scales, w, out_0, out_1, out_2):
+    nc = tc.nc
+    with ExitStack() as ctx:
+        keep = ctx.enter_context(tc.tile_pool(name="keep", bufs=1))
+        psum = ctx.enter_context(tc.psum_pool(name="psum", bufs=1))
+        ctx.enter_context(tc.manual_schedule(engines={mybir.EngineType.PE, mybir.EngineType.SP}))
+
+        def sb(name, shape, dtype):
+            return keep.tile([P] + shape, dtype, name=name, align_bytes=64)
+
+        banks = [psum.tile([P, BANK_COLS], F32, name="bank%d" % i) for i in range(BANKS)]
+        turn = [0]
+
+        def next_bank(among=BANKS):
+            turn[0] += 1
+            return banks[(turn[0] - 1) % among]
+
+        def span_of(spans, col):
+            return [i for i, (c0, n) in enumerate(spans) if c0 <= col < c0 + n][0]
+
+        gt_pairs = [(g, t) for g in range(OUT_PASSES) for t in range(PACK)]
+        ident = sb("ident", [P], F32)
+        w_raw = sb("w_raw", [OUT_PASSES, PACK], BF16)
+        w_pos = sb("w_pos", [OUT_PASSES * PACK], F32)
+        w_neg = sb("w_neg", [OUT_PASSES * PACK], F32)
+        g_raw = {gt: sb("g_raw%d%d" % gt, [N_IN], BF16) for gt in gt_pairs}
+        g_stage = [sb("g_grp%d" % t, [N_IN], BF16) for t in range(PACK)]
+        g_grp = {(g, t): g_stage[t] for g, t in gt_pairs}
+        g_codes = {gt: sb("g_codes%d%d" % gt, [IN_PASSES * P], U32) for gt in gt_pairs}
+        g_scales = {gt: sb("g_scales%d%d" % gt, [IN_PASSES * P], U8) for gt in gt_pairs}
+        l_raw = [sb("l_raw%d" % c, [OUT_PASSES, 2 * K_PASS], U8) for c in range(IN_PASSES)]
+        l_words = [sb("l_words%d" % c, [OUT_PASSES, 2 * K_PASS], U8) for c in range(IN_PASSES)]
+        ls_raw = sb("ls_raw", [OUT_PASSES, N_IN], U8)
+        l_scales = [sb("l_scales%d" % c, [OUT_PASSES, K_PASS], U8) for c in range(IN_PASSES)]
+        u_raw = {(s, c): sb("u_raw%d%d" % (s, c), [PACK, n], BF16) for s, (c0, n) in enumerate(LOAD_SPANS) for c in range(IN_PASSES)}
+        r_raw = {(s, g): sb("r_raw%d%d" % (s, g), [PACK, n], BF16) for s, (c0, n) in enumerate(LOAD_SPANS) for g in range(OUT_PASSES)}
+        pairs = range(TASKS // PAIR)
+        units = range(TASKS // UNIT)
+        u_grp = {(k, c): sb("u_grp%d%d" % (k, c), [PAIR * PACK], BF16) for k in pairs for c in range(IN_PASSES)}
+        u_codes = {(k, c): sb("u_codes%d%d" % (k, c), [PAIR], U32) for k in pairs for c in range(IN_PASSES)}
+        u_scales = {(k, c): sb("u_scales%d%d" % (k, c), [PAIR], U8) for k in pairs for c in range(IN_PASSES)}
+        y_f32 = {(s, g): sb("y_f32%d%d" % (s, g), [PACK, n], F32) for s, (c0, n) in enumerate(LAST_SPANS) for g in range(OUT_PASSES)}
+        e_stage = [sb("e_grp%d" % j, [OUT_PASSES * UNIT * PACK], BF16) for j in range(4)]
+        e_grp = [e_stage[j % 4] for j in units]
+        e_codes = [sb("e_codes%d" % j, [OUT_PASSES * UNIT], U32) for j in units]
+        e_scales = [sb("e_scales%d" % j, [OUT_PASSES * UNIT], U8) for j in units]
+        u1_codes = {(s, c): sb("u1_codes%d%d" % (s, c), [n], U32) for s, (c0, n) in enumerate(LAST_SPANS) for c in range(IN_PASSES)}
+        u1_scales = {(s, c): sb("u1_scales%d%d" % (s, c), [n], U8) for s, (c0, n) in enumerate(LAST_SPANS) for c in range(IN_PASSES)}
+        y_stage = [sb("y_grp%d" % i, [PAIR * PACK], BF16) for i in range(4)]
+        y_grp = {(s, g): y_stage[(2 * s + g) % 4][:, : n * PACK] for s, (c0, n) in enumerate(LAST_SPANS) for g in range(OUT_PASSES)}
+        y_codes = [sb("y_codes%d" % s, [OUT_PASSES, n], U32) for s, (c0, n) in enumerate(LAST_SPANS)]
+        y_scales = [sb("y_scales%d" % i, [OUT_PASSES, n], U8) for i, (c0, n) in enumerate(SCALE_SPANS)]
+
+        def load_g(g, t):
+            rows = plant[g * K_PASS : (g + 1) * K_PASS, :].rearrange("(m t) k -> m t k", t=PACK)
+            nc.sync.dma_start(out=g_raw[g, t][:], in_=rows[:, t, :])
+
+        def load_u(s, c):
+            c0, n = LOAD_SPANS[s]
+            rows = u[c * K_PASS : (c + 1) * K_PASS, c0 : c0 + n]
+            nc.sync.dma_start(out=u_raw[s, c][:], in_=rows.rearrange("(p t) m -> p t m", t=PACK))
+
+        def load_r(s, g):
+            c0, n = LOAD_SPANS[s]
+            rows = r[g * K_PASS : (g + 1) * K_PASS, c0 : c0 + n]
+            nc.sync.dma_start(out=r_raw[s, g][:], in_=rows.rearrange("(p t) m -> p t m", t=PACK))
+
+        def load_l(c):
+            cols = learn_words[:, :, 2 * c * K_PASS : 2 * (c + 1) * K_PASS]
+            nc.sync.dma_start(out=l_raw[c][:].bitcast(I32), in_=cols.rearrange("g p b -> p g b").bitcast(I32))
+
+        waiting = []
+        chores = []
+
+        def defer(key, lag, fn):
+            waiting.append([key, lag, fn])
+
+        def settle(key):
+            for item in [x for x in waiting if x[0] == key]:
+                waiting.remove(item)
+                item[2]()
+
+        def tick(n_chores=1):
+            for item in list(waiting):
+                item[1] -= 1
+                if item[1] < 0:
+                    waiting.remove(item)
+                    item[2]()
+            for fn in chores[:n_chores]:
+                chores.remove(fn)
+                fn()
+
+        def quantize(codes, scales, grouped):
+            nc.vector.quantize_mx(out=codes.bitcast(FP8X4), scales=scales, in_=grouped)
+
+        def interleaved(grouped):
+            return grouped.rearrange("p (c i t) -> p c t i", i=4, t=PACK)
+
+        def by_four(rows):
+            return rows.rearrange("p t (c i) -> p c t i", i=4)
+
+        def turn_g(g, t):
+            words = g_raw[g, t][:].bitcast(F32)
+            for c0, nc_here in G_PARTS:
+                bank = next_bank(TURN_BANKS)
+                for c in range(nc_here):
+                    for half in range(2):
+                        col = (c * 2 + half) * P
+                        first = (c0 + c) * 2 * P
+                        nc.tensor.transpose(bank[:, col : col + P], words[:, first + half : first + 2 * P : 2], ident[:])
+                dst = g_grp[g, t][:, c0 * K_PASS : (c0 + nc_here) * K_PASS].bitcast(F32)
+                src = bank[:, : nc_here * 2 * P]
+                nc.scalar.copy(out=dst.rearrange("p (c m v) -> p c m v", m=P, v=2), in_=src.rearrange("p (c v m) -> p c m v", m=P, v=2))
+
+        def quantize_g(g, t):
+            for c0, nc_here in G_PARTS:
+                cols = slice(c0 * P, (c0 + nc_here) * P)
+                quantize(g_codes[g, t][:, cols], g_scales[g, t][:, cols], g_grp[g, t][:, c0 * K_PASS : (c0 + nc_here) * K_PASS])
+
+        def u_rows(k, c):
+            s = span_of(LOAD_SPANS, k * PAIR)
+            off = k * PAIR - LOAD_SPANS[s][0]
+            return u_raw[s, c][:, :, off : off + PAIR]
+
+        def group_u_vector(k, c):
+            nc.vector.tensor_copy(out=interleaved(u_grp[k, c][:]), in_=by_four(u_rows(k, c)))
+
+        def quantize_u(k, c):
+            quantize(u_codes[k, c][:], u_scales[k, c][:], u_grp[k, c][:])
+
+        def group_u(k, c):
+            nc.scalar.copy(out=interleaved(u_grp[k, c][:]), in_=by_four(u_rows(k, c)))
+            defer(("u", k), 4, lambda: quantize_u(k, c))
+
+        def weigh_r(s, g):
+            c0, n = LAST_SPANS[s]
+            ls = span_of(LOAD_SPANS, c0)
+            off = c0 - LOAD_SPANS[ls][0]
+            for t in range(PACK):
+                col = g * PACK + t
+                nc.scalar.activation(out=y_f32[s, g][:, t, :], in_=r_raw[ls, g][:, t, off : off + n], func=ACT.Copy, scale=w_pos[:, col : col + 1])
+
+        def order_l_words(c, g):
+            nc.vector.tensor_copy(
+                out=l_words[c][:, g, :].rearrange("p (t m b) -> p t m b", t=PACK, b=2),
+                in_=l_raw[c][:, g, :].rearrange("p (m t b) -> p t m b", t=PACK, b=2),
+            )
+
+        def order_l_scales(c):
+            nc.vector.tensor_copy(
+                out=l_scales[c][:].rearrange("p g (t m) -> p g t m", t=PACK),
+                in_=ls_raw[:, :, c * K_PASS : (c + 1) * K_PASS].rearrange("p g (m t) -> p g t m", t=PACK),
+            )
+
+        def error_now_sums(bank, j, g, t):
+            k, off = divmod(j * UNIT, PAIR)
+            for c in range(IN_PASSES):
+                nc.tensor.matmul_mx(
+                    out=bank[:, t * P : (t + 1) * P],
+                    lhsT=g_codes[g, t][:, c * P : (c + 1) * P].bitcast(FP8X4),
+                    lhsT_scale=g_scales[g, t][:, c * P : (c + 1) * P],
+                    rhs=u_codes[k, c][:, off : off + UNIT].bitcast(FP8X4),
+                    rhs_scale=u_scales[k, c][:, off : off + UNIT],
+                    start=(c == 0),
+                    stop=(c == IN_PASSES - 1),
+                )
+
+        def error_now(j, g):
+            settle(("u", j * UNIT // PAIR))
+            bank = next_bank()
+            for t in range(PACK):
+                error_now_sums(bank, j, g, t)
+            error_now_out(bank, j, g)
+
+        def error_now_out(bank, j, g):
+            s = span_of(LOAD_SPANS, j * UNIT)
+            roff = j * UNIT - LOAD_SPANS[s][0]
+            nc.vector.tensor_tensor(
+                out=interleaved(e_grp[j][:, g * K_PASS : (g + 1) * K_PASS]),
+                in0=by_four(r_raw[s, g][:, :, roff : roff + UNIT]),
+                in1=by_four(bank[:].rearrange("p (t m) -> p t m", t=PACK)),
+                op=ALU.subtract,
+            )
+            tick()
+            if g == OUT_PASSES - 1:
+                defer(("e", j), 0, lambda: quantize(e_codes[j][:], e_scales[j][:], e_grp[j][:]))
+
+        def learn(j, c):
+            settle(("e", j))
+            settle(("l", c))
+            bank = next_bank()
+            for t in range(PACK):
+                for g in range(OUT_PASSES):
+                    nc.tensor.matmul_mx(
+                        out=bank[:, t * P : (t + 1) * P],
+                        lhsT=l_words[c][:, g, 2 * t * P : 2 * (t + 1) * P].bitcast(FP4X4),
+                        lhsT_scale=l_scales[c][:, g, t * P : (t + 1) * P],
+                        rhs=e_codes[j][:, g * UNIT : (g + 1) * UNIT].bitcast(FP8X4),
+                        rhs_scale=e_scales[j][:, g * UNIT : (g + 1) * UNIT],
+                        start=(g == 0),
+                        stop=(g == OUT_PASSES - 1),
+                    )
+            k, off = divmod(j * UNIT, PAIR)
+            s = span_of(LAST_SPANS, j * UNIT)
+            c0, n = LAST_SPANS[s]
+            soff = j * UNIT - c0
+            u_here = u_grp[k, c][:, off * PACK : (off + UNIT) * PACK].rearrange("p (m t) -> p m t", t=PACK)
+            u_span = u_grp[k, c][:, (c0 % PAIR) * PACK : (c0 % PAIR + n) * PACK]
+            nc.vector.tensor_tensor(
+                out=u_here,
+                in0=u_here,
+                in1=bank[:].rearrange("p (t m) -> p m t", t=PACK),
+                op=ALU.add,
+            )
+            tick()
+            if soff + UNIT == n:
+                defer(("u1", s), 0, lambda: quantize(u1_codes[s, c][:], u1_scales[s, c][:], u_span))
+
+        def store_y_scales(i):
+            c0, n = SCALE_SPANS[i]
+            for q in range(4):
+                engine = nc.scalar if q % 2 and c0 + n == TASKS else nc.sync
+                engine.dma_start(
+                    out=out_2[:, 4 * q : 4 * q + 4, c0 : c0 + n].rearrange("g r n -> r g n").bitcast(I32),
+                    in_=y_scales[i][32 * q : 32 * q + 4, :, :].bitcast(I32),
+                )
+
+        def quantize_y(s, g):
+            c0, n = LAST_SPANS[s]
+            i = span_of(SCALE_SPANS, c0)
+            off = c0 - SCALE_SPANS[i][0]
+            quantize(y_codes[s][:, g, :], y_scales[i][:, g, off : off + n], y_grp[s, g])
+            dst = out_1[g, :, c0 : c0 + n, :].rearrange("p m t -> p (m t)")
+            nc.sync.dma_start(out=dst.bitcast(I32), in_=y_codes[s][:, g, :].bitcast(I32))
+            if g == OUT_PASSES - 1 and off + n == SCALE_SPANS[i][1]:
+                store_y_scales(i)
+
+        def error_next(s, g):
+            settle(("u1", s))
+            c0, n = LAST_SPANS[s]
+            per_bank = BANK_COLS // n
+            for t0 in range(0, PACK, per_bank):
+                bank = next_bank()
+                for i in range(per_bank):
+                    t = t0 + i
+                    for c in range(IN_PASSES):
+                        nc.tensor.matmul_mx(
+                            out=bank[:, i * n : (i + 1) * n],
+                            lhsT=g_codes[g, t][:, c * P : (c + 1) * P].bitcast(FP8X4),
+                            lhsT_scale=g_scales[g, t][:, c * P : (c + 1) * P],
+                            rhs=u1_codes[s, c][:].bitcast(FP8X4),
+                            rhs_scale=u1_scales[s, c][:],
+                            start=(c == 0),
+                            stop=(c == IN_PASSES - 1),
+                        )
+                for i in range(per_bank):
+                    t = t0 + i
+                    col = g * PACK + t
+                    nc.vector.scalar_tensor_tensor(
+                        out=y_f32[s, g][:, t, :],
+                        in0=bank[:, i * n : (i + 1) * n],
+                        scalar=w_neg[:, col : col + 1],
+                        in1=y_f32[s, g][:, t, :],
+                        op0=ALU.mult,
+                        op1=ALU.add,
+                    )
+                if t0 + per_bank == PACK:
+                    y_rows = y_f32[s, g][:]
+                    nc.scalar.copy(out=interleaved(y_grp[s, g]), in_=by_four(y_rows))
+                    dst = out_0[g * K_PASS : (g + 1) * K_PASS, c0 : c0 + n].rearrange("(p t) m -> p t m", t=PACK)
+                    nc.sync.dma_start(out=dst, in_=y_rows)
+                tick()
+            defer(("y", s, g), 2, lambda: quantize_y(s, g))
+
+        make_identity(nc, ident[:])
+        nc.vector.memset(ls_raw[:].rearrange("p g n -> p (g n)").bitcast(I32), 0)
+        nc.scalar.dma_start(out=w_raw[:], in_=w.rearrange("(g p t) o -> p g (t o)", g=OUT_PASSES, t=PACK))
+        for q in range(4):
+            nc.scalar.dma_start(
+                out=ls_raw[32 * q : 32 * q + 4, :, :].bitcast(I32),
+                in_=learn_scales[:, 4 * q : 4 * q + 4, :].rearrange("g r n -> r g n").bitcast(I32),
+            )
+        load_g(0, 0)
+        load_g(0, 1)
+        load_g(0, 2)
+        load_g(0, 3)
+        load_u(0, 0)
+        load_u(0, 1)
+        load_u(0, 2)
+        load_g(1, 0)
+        load_g(1, 1)
+        load_g(1, 2)
+        load_g(1, 3)
+        load_r(0, 0)
+        load_l(0)
+        load_r(0, 1)
+        load_l(1)
+        load_u(1, 0)
+        load_u(1, 1)
+        load_u(1, 2)
+        load_l(2)
+        load_r(1, 0)
+        load_r(1, 1)
+        load_u(2, 0)
+        load_u(2, 1)
+        load_u(2, 2)
+        load_r(2, 0)
+        load_r(2, 1)
+
+        w_flat = w_raw[:].rearrange("p g t -> p (g t)")
+        nc.scalar.activation(out=w_pos[:], in_=w_flat, func=ACT.Copy, scale=1.0)
+        nc.scalar.activation(out=w_neg[:], in_=w_flat, func=ACT.Copy, scale=-1.0)
+
+        def first_sums(i):
+            settle(("u", 0))
+            g, t = gt_pairs[i]
+            for j in range(2):
+                error_now_sums(banks[TURN_BANKS + 2 * g + j], j, g, t)
+
+        turn_g(*gt_pairs[0])
+        order_l_scales(0)
+        order_l_scales(1)
+        order_l_scales(2)
+        turn_g(*gt_pairs[1])
+        quantize_g(*gt_pairs[0])
+        turn_g(*gt_pairs[2])
+        quantize_g(*gt_pairs[1])
+        turn_g(*gt_pairs[3])
+        quantize_g(*gt_pairs[2])
+        group_u(0, 0)
+        quantize_g(*gt_pairs[3])
+        group_u(0, 1)
+        turn_g(*gt_pairs[4])
+        group_u_vector(0, 2)
+        quantize_u(0, 2)
+        first_sums(0)
+        first_sums(1)
+        first_sums(2)
+        first_sums(3)
+        quantize_g(*gt_pairs[4])
+        order_l_words(0, 0)
+        turn_g(*gt_pairs[5])
+        turn_g(*gt_pairs[6])
+        turn_g(*gt_pairs[7])
+        quantize_g(*gt_pairs[5])
+        order_l_words(0, 1)
+        quantize_g(*gt_pairs[6])
+        error_now_out(banks[TURN_BANKS + 2 * 0 + 0], 0, 0)
+        quantize_g(*gt_pairs[7])
+        error_now_out(banks[TURN_BANKS + 2 * 0 + 1], 1, 0)
+        first_sums(4)
+        first_sums(5)
+        first_sums(6)
+        first_sums(7)
+        group_u(1, 0)
+        group_u(1, 1)
+        group_u(1, 2)
+        error_now_out(banks[TURN_BANKS + 2 * 1 + 0], 0, 1)
+        error_now_out(banks[TURN_BANKS + 2 * 1 + 1], 1, 1)
+        defer(("l", 1), 3, lambda: order_l_words(1, 0))
+        defer(("l", 1), 4, lambda: order_l_words(1, 1))
+        defer(("l", 2), 5, lambda: order_l_words(2, 0))
+        defer(("l", 2), 6, lambda: order_l_words(2, 1))
+        for k in range(2, len(pairs)):
+            chores.extend([lambda k=k, c=c: group_u(k, c) for c in range(IN_PASSES)])
+            chores.extend([lambda k=k, g=g: weigh_r(k - 2, g) for g in range(OUT_PASSES)])
+        for s in range(2, len(LAST_SPANS)):
+            chores.extend([lambda s=s, g=g: weigh_r(s, g) for g in range(OUT_PASSES)])
+        turn[0] = 0
+
+        def stage1(j):
+            for g in range(OUT_PASSES):
+                error_now(j, g)
+
+        def stage2(j):
+            for c in range(IN_PASSES):
+                learn(j, c)
+
+        def stage3(s):
+            for g in range(OUT_PASSES):
+                error_next(s, g)
+
+        for step, i in ORDER:
+            [stage1, stage2, stage3][step - 1](i)
+        for item in list(waiting):
+            item[2]()

@@ -26,7 +26,10 @@ BANK_COLS = 512
 UNIT = 128
 PAIR = 256
 TURN_BANKS = 4
-G_PARTS = [(0, 2), (2, 1)]
+U_LAG = 3
+Y_LAG = 4
+FUSED = [3, 4]
+PARTS = [(0, 2), (2, 1)]
 ORDER = [(2, 0), (2, 1), (1, 2), (1, 3), (3, 0), (2, 2), (1, 4), (2, 3), (1, 5), (2, 4), (3, 1), (1, 6), (2, 5), (1, 7), (2, 6), (3, 2), (2, 7), (3, 3), (3, 4)]
 SCALE_SPANS = [(0, 768), (768, 256)]
 LOAD_SPANS = [(0, 256), (256, 256), (512, 512)]
@@ -59,10 +62,9 @@ def tile_lifted_learning_control_error_k1_kernel(tc, u, r, plant, learn_words, l
         w_pos = sb("w_pos", [OUT_PASSES * PACK], F32)
         w_neg = sb("w_neg", [OUT_PASSES * PACK], F32)
         g_raw = {gt: sb("g_raw%d%d" % gt, [N_IN], BF16) for gt in gt_pairs}
-        g_stage = [sb("g_grp%d" % t, [N_IN], BF16) for t in range(PACK)]
-        g_grp = {(g, t): g_stage[t] for g, t in gt_pairs}
-        g_codes = {gt: sb("g_codes%d%d" % gt, [IN_PASSES * P], U32) for gt in gt_pairs}
-        g_scales = {gt: sb("g_scales%d%d" % gt, [IN_PASSES * P], U8) for gt in gt_pairs}
+        g_stage = [sb("g_grp%d" % i, [2 * N_IN], BF16) for i in range(2)]
+        g_codes = [sb("g_codes%d" % i, [2 * IN_PASSES * P], U32) for i in range(PACK)]
+        g_scales = [sb("g_scales%d" % i, [2 * IN_PASSES * P], U8) for i in range(PACK)]
         l_raw = [sb("l_raw%d" % c, [OUT_PASSES, 2 * K_PASS], U8) for c in range(IN_PASSES)]
         l_words = [sb("l_words%d" % c, [OUT_PASSES, 2 * K_PASS], U8) for c in range(IN_PASSES)]
         ls_raw = sb("ls_raw", [OUT_PASSES, N_IN], U8)
@@ -71,16 +73,16 @@ def tile_lifted_learning_control_error_k1_kernel(tc, u, r, plant, learn_words, l
         r_raw = {(s, g): sb("r_raw%d%d" % (s, g), [PACK, n], BF16) for s, (c0, n) in enumerate(LOAD_SPANS) for g in range(OUT_PASSES)}
         pairs = range(TASKS // PAIR)
         units = range(TASKS // UNIT)
-        u_grp = {(k, c): sb("u_grp%d%d" % (k, c), [PAIR * PACK], BF16) for k in pairs for c in range(IN_PASSES)}
-        u_codes = {(k, c): sb("u_codes%d%d" % (k, c), [PAIR], U32) for k in pairs for c in range(IN_PASSES)}
-        u_scales = {(k, c): sb("u_scales%d%d" % (k, c), [PAIR], U8) for k in pairs for c in range(IN_PASSES)}
+        u_grp = [sb("u_grp%d" % k, [IN_PASSES * PAIR * PACK], BF16) for k in pairs]
+        u_codes = [sb("u_codes%d" % k, [IN_PASSES * PAIR], U32) for k in pairs]
+        u_scales = [sb("u_scales%d" % k, [IN_PASSES * PAIR], U8) for k in pairs]
         y_f32 = {(s, g): sb("y_f32%d%d" % (s, g), [PACK, n], F32) for s, (c0, n) in enumerate(LAST_SPANS) for g in range(OUT_PASSES)}
         e_stage = [sb("e_grp%d" % j, [OUT_PASSES * UNIT * PACK], BF16) for j in range(4)]
         e_grp = [e_stage[j % 4] for j in units]
         e_codes = [sb("e_codes%d" % j, [OUT_PASSES * UNIT], U32) for j in units]
         e_scales = [sb("e_scales%d" % j, [OUT_PASSES * UNIT], U8) for j in units]
-        u1_codes = {(s, c): sb("u1_codes%d%d" % (s, c), [n], U32) for s, (c0, n) in enumerate(LAST_SPANS) for c in range(IN_PASSES)}
-        u1_scales = {(s, c): sb("u1_scales%d%d" % (s, c), [n], U8) for s, (c0, n) in enumerate(LAST_SPANS) for c in range(IN_PASSES)}
+        u1_codes = [sb("u1_codes%d" % s, [IN_PASSES * n], U32) for s, (c0, n) in enumerate(LAST_SPANS)]
+        u1_scales = [sb("u1_scales%d" % s, [IN_PASSES * n], U8) for s, (c0, n) in enumerate(LAST_SPANS)]
         y_stage = [sb("y_grp%d" % i, [PAIR * PACK], BF16) for i in range(4)]
         y_grp = {(s, g): y_stage[(2 * s + g) % 4][:, : n * PACK] for s, (c0, n) in enumerate(LAST_SPANS) for g in range(OUT_PASSES)}
         y_codes = [sb("y_codes%d" % s, [OUT_PASSES, n], U32) for s, (c0, n) in enumerate(LAST_SPANS)]
@@ -134,51 +136,64 @@ def tile_lifted_learning_control_error_k1_kernel(tc, u, r, plant, learn_words, l
         def by_four(rows):
             return rows.rearrange("p t (c i) -> p c t i", i=4)
 
-        def turn_g(g, t):
-            words = g_raw[g, t][:].bitcast(F32)
-            for c0, nc_here in G_PARTS:
+        def turn_g(i):
+            g, h = divmod(i, 2)
+            for b in range(3):
                 bank = next_bank(TURN_BANKS)
-                for c in range(nc_here):
+                for x in range(2):
+                    t, c = divmod(2 * b + x, IN_PASSES)
+                    words = g_raw[g, 2 * h + t][:].bitcast(F32)
                     for half in range(2):
-                        col = (c * 2 + half) * P
-                        first = (c0 + c) * 2 * P
-                        nc.tensor.transpose(bank[:, col : col + P], words[:, first + half : first + 2 * P : 2], ident[:])
-                dst = g_grp[g, t][:, c0 * K_PASS : (c0 + nc_here) * K_PASS].bitcast(F32)
-                src = bank[:, : nc_here * 2 * P]
-                nc.scalar.copy(out=dst.rearrange("p (c m v) -> p c m v", m=P, v=2), in_=src.rearrange("p (c v m) -> p c m v", m=P, v=2))
+                        col = (x * 2 + half) * P
+                        nc.tensor.transpose(bank[:, col : col + P], words[:, c * 2 * P + half : (c + 1) * 2 * P : 2], ident[:])
+                dst = g_stage[h][:, b * 2 * K_PASS : (b + 1) * 2 * K_PASS].bitcast(F32)
+                nc.scalar.copy(out=dst.rearrange("p (x m v) -> p x m v", m=P, v=2), in_=bank[:].rearrange("p (x v m) -> p x m v", m=P, v=2))
 
-        def quantize_g(g, t):
-            for c0, nc_here in G_PARTS:
-                cols = slice(c0 * P, (c0 + nc_here) * P)
-                quantize(g_codes[g, t][:, cols], g_scales[g, t][:, cols], g_grp[g, t][:, c0 * K_PASS : (c0 + nc_here) * K_PASS])
+        def quantize_g(i, part):
+            b0, nb = PARTS[part]
+            cols = slice(b0 * 2 * P, (b0 + nb) * 2 * P)
+            quantize(g_codes[i][:, cols], g_scales[i][:, cols], g_stage[i % 2][:, b0 * 2 * K_PASS : (b0 + nb) * 2 * K_PASS])
+
+        def g_operand(g, t, c):
+            i = 2 * g + t // 2
+            cols = slice(((t % 2) * IN_PASSES + c) * P, ((t % 2) * IN_PASSES + c + 1) * P)
+            return g_codes[i][:, cols].bitcast(FP8X4), g_scales[i][:, cols]
 
         def u_rows(k, c):
             s = span_of(LOAD_SPANS, k * PAIR)
             off = k * PAIR - LOAD_SPANS[s][0]
             return u_raw[s, c][:, :, off : off + PAIR]
 
-        def group_u_vector(k, c):
-            nc.vector.tensor_copy(out=interleaved(u_grp[k, c][:]), in_=by_four(u_rows(k, c)))
+        def u_pass(k, c):
+            return u_grp[k][:, c * PAIR * PACK : (c + 1) * PAIR * PACK]
 
-        def quantize_u(k, c):
-            quantize(u_codes[k, c][:], u_scales[k, c][:], u_grp[k, c][:])
+        def group_u_vector(k, c):
+            nc.vector.tensor_copy(out=interleaved(u_pass(k, c)), in_=by_four(u_rows(k, c)))
+
+        def quantize_u(k, part):
+            c0, n = PARTS[part]
+            cols = slice(c0 * PAIR, (c0 + n) * PAIR)
+            quantize(u_codes[k][:, cols], u_scales[k][:, cols], u_grp[k][:, c0 * PAIR * PACK : (c0 + n) * PAIR * PACK])
 
         def group_u(k, c):
-            nc.scalar.copy(out=interleaved(u_grp[k, c][:]), in_=by_four(u_rows(k, c)))
-            defer(("u", k), 4, lambda: quantize_u(k, c))
+            nc.scalar.copy(out=interleaved(u_pass(k, c)), in_=by_four(u_rows(k, c)))
+            if c > 0:
+                defer(("u", k), U_LAG, lambda: quantize_u(k, c - 1))
 
-        def weigh_r(s, g):
-            c0, n = LAST_SPANS[s]
-            ls = span_of(LOAD_SPANS, c0)
-            off = c0 - LOAD_SPANS[ls][0]
+        def r_rows(g, c0, n):
+            s = span_of(LOAD_SPANS, c0)
+            off = c0 - LOAD_SPANS[s][0]
+            return r_raw[s, g][:, :, off : off + n]
+
+        def weigh(s, g, rows):
             for t in range(PACK):
                 col = g * PACK + t
-                nc.scalar.activation(out=y_f32[s, g][:, t, :], in_=r_raw[ls, g][:, t, off : off + n], func=ACT.Copy, scale=w_pos[:, col : col + 1])
+                nc.scalar.activation(out=y_f32[s, g][:, t, :], in_=rows[:, t, :], func=ACT.Copy, scale=w_pos[:, col : col + 1])
 
-        def order_l_words(c, g):
+        def order_l_words(c):
             nc.vector.tensor_copy(
-                out=l_words[c][:, g, :].rearrange("p (t m b) -> p t m b", t=PACK, b=2),
-                in_=l_raw[c][:, g, :].rearrange("p (m t b) -> p t m b", t=PACK, b=2),
+                out=l_words[c][:].rearrange("p g (t m b) -> p g t m b", t=PACK, b=2),
+                in_=l_raw[c][:].rearrange("p g (m t b) -> p g t m b", t=PACK, b=2),
             )
 
         def order_l_scales(c):
@@ -192,10 +207,10 @@ def tile_lifted_learning_control_error_k1_kernel(tc, u, r, plant, learn_words, l
             for c in range(IN_PASSES):
                 nc.tensor.matmul_mx(
                     out=bank[:, t * P : (t + 1) * P],
-                    lhsT=g_codes[g, t][:, c * P : (c + 1) * P].bitcast(FP8X4),
-                    lhsT_scale=g_scales[g, t][:, c * P : (c + 1) * P],
-                    rhs=u_codes[k, c][:, off : off + UNIT].bitcast(FP8X4),
-                    rhs_scale=u_scales[k, c][:, off : off + UNIT],
+                    lhsT=g_operand(g, t, c)[0],
+                    lhsT_scale=g_operand(g, t, c)[1],
+                    rhs=u_codes[k][:, c * PAIR + off : c * PAIR + off + UNIT].bitcast(FP8X4),
+                    rhs_scale=u_scales[k][:, c * PAIR + off : c * PAIR + off + UNIT],
                     start=(c == 0),
                     stop=(c == IN_PASSES - 1),
                 )
@@ -208,11 +223,9 @@ def tile_lifted_learning_control_error_k1_kernel(tc, u, r, plant, learn_words, l
             error_now_out(bank, j, g)
 
         def error_now_out(bank, j, g):
-            s = span_of(LOAD_SPANS, j * UNIT)
-            roff = j * UNIT - LOAD_SPANS[s][0]
             nc.vector.tensor_tensor(
                 out=interleaved(e_grp[j][:, g * K_PASS : (g + 1) * K_PASS]),
-                in0=by_four(r_raw[s, g][:, :, roff : roff + UNIT]),
+                in0=by_four(r_rows(g, j * UNIT, UNIT)),
                 in1=by_four(bank[:].rearrange("p (t m) -> p t m", t=PACK)),
                 op=ALU.subtract,
             )
@@ -239,8 +252,7 @@ def tile_lifted_learning_control_error_k1_kernel(tc, u, r, plant, learn_words, l
             s = span_of(LAST_SPANS, j * UNIT)
             c0, n = LAST_SPANS[s]
             soff = j * UNIT - c0
-            u_here = u_grp[k, c][:, off * PACK : (off + UNIT) * PACK].rearrange("p (m t) -> p m t", t=PACK)
-            u_span = u_grp[k, c][:, (c0 % PAIR) * PACK : (c0 % PAIR + n) * PACK]
+            u_here = u_pass(k, c)[:, off * PACK : (off + UNIT) * PACK].rearrange("p (m t) -> p m t", t=PACK)
             nc.vector.tensor_tensor(
                 out=u_here,
                 in0=u_here,
@@ -248,8 +260,14 @@ def tile_lifted_learning_control_error_k1_kernel(tc, u, r, plant, learn_words, l
                 op=ALU.add,
             )
             tick()
-            if soff + UNIT == n:
-                defer(("u1", s), 0, lambda: quantize(u1_codes[s, c][:], u1_scales[s, c][:], u_span))
+            if n == UNIT:
+                src = u_pass(k, c)[:, off * PACK : (off + UNIT) * PACK]
+                defer(("u1", s), 0, lambda: quantize(u1_codes[s][:, c * n : (c + 1) * n], u1_scales[s][:, c * n : (c + 1) * n], src))
+            elif soff + UNIT == n and c > 0:
+                first, count = PARTS[c - 1]
+                cols = slice(first * n, (first + count) * n)
+                src = u_grp[k][:, first * n * PACK : (first + count) * n * PACK]
+                defer(("u1", s), 0, lambda: quantize(u1_codes[s][:, cols], u1_scales[s][:, cols], src))
 
         def store_y_scales(i):
             c0, n = SCALE_SPANS[i]
@@ -281,31 +299,41 @@ def tile_lifted_learning_control_error_k1_kernel(tc, u, r, plant, learn_words, l
                     for c in range(IN_PASSES):
                         nc.tensor.matmul_mx(
                             out=bank[:, i * n : (i + 1) * n],
-                            lhsT=g_codes[g, t][:, c * P : (c + 1) * P].bitcast(FP8X4),
-                            lhsT_scale=g_scales[g, t][:, c * P : (c + 1) * P],
-                            rhs=u1_codes[s, c][:].bitcast(FP8X4),
-                            rhs_scale=u1_scales[s, c][:],
+                            lhsT=g_operand(g, t, c)[0],
+                            lhsT_scale=g_operand(g, t, c)[1],
+                            rhs=u1_codes[s][:, c * n : (c + 1) * n].bitcast(FP8X4),
+                            rhs_scale=u1_scales[s][:, c * n : (c + 1) * n],
                             start=(c == 0),
                             stop=(c == IN_PASSES - 1),
                         )
-                for i in range(per_bank):
-                    t = t0 + i
-                    col = g * PACK + t
-                    nc.vector.scalar_tensor_tensor(
-                        out=y_f32[s, g][:, t, :],
-                        in0=bank[:, i * n : (i + 1) * n],
-                        scalar=w_neg[:, col : col + 1],
-                        in1=y_f32[s, g][:, t, :],
-                        op0=ALU.mult,
-                        op1=ALU.add,
+                if s in FUSED:
+                    for i in range(per_bank):
+                        t = t0 + i
+                        col = g * PACK + t
+                        nc.vector.scalar_tensor_tensor(
+                            out=y_f32[s, g][:, t, :],
+                            in0=bank[:, i * n : (i + 1) * n],
+                            scalar=w_neg[:, col : col + 1],
+                            in1=y_f32[s, g][:, t, :],
+                            op0=ALU.mult,
+                            op1=ALU.add,
+                        )
+                else:
+                    nc.vector.tensor_tensor(
+                        out=y_f32[s, g][:, t0 : t0 + per_bank, :],
+                        in0=r_rows(g, c0, n)[:, t0 : t0 + per_bank, :],
+                        in1=bank[:].rearrange("p (t m) -> p t m", t=per_bank),
+                        op=ALU.subtract,
                     )
                 if t0 + per_bank == PACK:
+                    if s not in FUSED:
+                        weigh(s, g, y_f32[s, g])
                     y_rows = y_f32[s, g][:]
                     nc.scalar.copy(out=interleaved(y_grp[s, g]), in_=by_four(y_rows))
                     dst = out_0[g * K_PASS : (g + 1) * K_PASS, c0 : c0 + n].rearrange("(p t) m -> p t m", t=PACK)
                     nc.sync.dma_start(out=dst, in_=y_rows)
                 tick()
-            defer(("y", s, g), 2, lambda: quantize_y(s, g))
+            defer(("y", s, g), Y_LAG, lambda: quantize_y(s, g))
 
         make_identity(nc, ident[:])
         nc.vector.memset(ls_raw[:].rearrange("p g n -> p (g n)").bitcast(I32), 0)
@@ -315,25 +343,25 @@ def tile_lifted_learning_control_error_k1_kernel(tc, u, r, plant, learn_words, l
                 out=ls_raw[32 * q : 32 * q + 4, :, :].bitcast(I32),
                 in_=learn_scales[:, 4 * q : 4 * q + 4, :].rearrange("g r n -> r g n").bitcast(I32),
             )
-        load_g(0, 0)
-        load_g(0, 1)
-        load_g(0, 2)
-        load_g(0, 3)
         load_u(0, 0)
         load_u(0, 1)
         load_u(0, 2)
+        load_g(0, 0)
+        load_g(0, 1)
+        load_l(0)
+        load_g(0, 2)
+        load_g(0, 3)
+        load_r(0, 0)
         load_g(1, 0)
         load_g(1, 1)
+        load_l(1)
         load_g(1, 2)
         load_g(1, 3)
-        load_r(0, 0)
-        load_l(0)
         load_r(0, 1)
-        load_l(1)
+        load_l(2)
         load_u(1, 0)
         load_u(1, 1)
         load_u(1, 2)
-        load_l(2)
         load_r(1, 0)
         load_r(1, 1)
         load_u(2, 0)
@@ -352,39 +380,36 @@ def tile_lifted_learning_control_error_k1_kernel(tc, u, r, plant, learn_words, l
             for j in range(2):
                 error_now_sums(banks[TURN_BANKS + 2 * g + j], j, g, t)
 
-        turn_g(*gt_pairs[0])
         order_l_scales(0)
         order_l_scales(1)
         order_l_scales(2)
-        turn_g(*gt_pairs[1])
-        quantize_g(*gt_pairs[0])
-        turn_g(*gt_pairs[2])
-        quantize_g(*gt_pairs[1])
-        turn_g(*gt_pairs[3])
-        quantize_g(*gt_pairs[2])
+        turn_g(0)
         group_u(0, 0)
-        quantize_g(*gt_pairs[3])
-        group_u(0, 1)
-        turn_g(*gt_pairs[4])
+        group_u_vector(0, 1)
+        quantize_u(0, 0)
         group_u_vector(0, 2)
-        quantize_u(0, 2)
+        quantize_u(0, 1)
+        quantize_g(0, 0)
+        quantize_g(0, 1)
+        turn_g(1)
+        settle(("u", 0))
         first_sums(0)
         first_sums(1)
+        quantize_g(1, 0)
+        quantize_g(1, 1)
+        turn_g(2)
         first_sums(2)
         first_sums(3)
-        quantize_g(*gt_pairs[4])
-        order_l_words(0, 0)
-        turn_g(*gt_pairs[5])
-        turn_g(*gt_pairs[6])
-        turn_g(*gt_pairs[7])
-        quantize_g(*gt_pairs[5])
-        order_l_words(0, 1)
-        quantize_g(*gt_pairs[6])
+        quantize_g(2, 0)
+        quantize_g(2, 1)
+        order_l_words(0)
+        turn_g(3)
         error_now_out(banks[TURN_BANKS + 2 * 0 + 0], 0, 0)
-        quantize_g(*gt_pairs[7])
         error_now_out(banks[TURN_BANKS + 2 * 0 + 1], 1, 0)
         first_sums(4)
         first_sums(5)
+        quantize_g(3, 0)
+        quantize_g(3, 1)
         first_sums(6)
         first_sums(7)
         group_u(1, 0)
@@ -392,15 +417,12 @@ def tile_lifted_learning_control_error_k1_kernel(tc, u, r, plant, learn_words, l
         group_u(1, 2)
         error_now_out(banks[TURN_BANKS + 2 * 1 + 0], 0, 1)
         error_now_out(banks[TURN_BANKS + 2 * 1 + 1], 1, 1)
-        defer(("l", 1), 3, lambda: order_l_words(1, 0))
-        defer(("l", 1), 4, lambda: order_l_words(1, 1))
-        defer(("l", 2), 5, lambda: order_l_words(2, 0))
-        defer(("l", 2), 6, lambda: order_l_words(2, 1))
+        defer(("l", 1), 1, lambda: order_l_words(1))
+        defer(("l", 2), 2, lambda: order_l_words(2))
         for k in range(2, len(pairs)):
             chores.extend([lambda k=k, c=c: group_u(k, c) for c in range(IN_PASSES)])
-            chores.extend([lambda k=k, g=g: weigh_r(k - 2, g) for g in range(OUT_PASSES)])
-        for s in range(2, len(LAST_SPANS)):
-            chores.extend([lambda s=s, g=g: weigh_r(s, g) for g in range(OUT_PASSES)])
+        for s in FUSED:
+            chores.extend([lambda s=s, g=g: weigh(s, g, r_rows(g, *LAST_SPANS[s])) for g in range(OUT_PASSES)])
         turn[0] = 0
 
         def stage1(j):

@@ -21,19 +21,23 @@ PACK = 4
 K_PASS = P * PACK
 IN_PASSES = N_IN // K_PASS
 OUT_PASSES = N_OUT // K_PASS
+QUADRANTS = 4
 BANKS = 8
 BANK_COLS = 512
-UNIT = 128
-PAIR = 256
 TURN_BANKS = 4
-U_LAG = 3
-Y_LAG = 4
-FUSED = [3, 4]
-PARTS = [(0, 2), (2, 1)]
-ORDER = [(2, 0), (2, 1), (1, 2), (1, 3), (3, 0), (2, 2), (1, 4), (2, 3), (1, 5), (2, 4), (3, 1), (1, 6), (2, 5), (1, 7), (2, 6), (3, 2), (2, 7), (3, 3), (3, 4)]
-SCALE_SPANS = [(0, 768), (768, 256)]
+
+UNIT = 128
+PAIR = 2 * UNIT
 LOAD_SPANS = [(0, 256), (256, 256), (512, 512)]
-LAST_SPANS = [(0, 256), (256, 256), (512, 256), (768, 128), (896, 128)]
+Y_SPANS = [(0, 256), (256, 256), (512, 256), (768, 128), (896, 128)]
+SCALE_SPANS = [(0, 512), (512, 512)]
+PARTS = [(0, 2), (2, 1)]
+
+U_LAG = 3
+Y_LAG_WIDE = 7
+Y_LAG_NARROW = 3
+E_TILES, U1_TILES, Y_TILES = 4, 3, 4
+WARM_FIRST, WARM_SECOND = 10, 16
 
 
 def tile_lifted_learning_control_error_k1_kernel(tc, u, r, plant, learn_words, learn_scales, w, out_0, out_1, out_2):
@@ -41,201 +45,226 @@ def tile_lifted_learning_control_error_k1_kernel(tc, u, r, plant, learn_words, l
     with ExitStack() as ctx:
         keep = ctx.enter_context(tc.tile_pool(name="keep", bufs=1))
         psum = ctx.enter_context(tc.psum_pool(name="psum", bufs=1))
-        ctx.enter_context(tc.manual_schedule(engines={mybir.EngineType.PE, mybir.EngineType.SP}))
+        ctx.enter_context(tc.manual_schedule())
 
         def sb(name, shape, dtype):
             return keep.tile([P] + shape, dtype, name=name, align_bytes=64)
 
+        def span_of(spans, task):
+            return [i for i, (first, count) in enumerate(spans) if first <= task < first + count][0]
+
         banks = [psum.tile([P, BANK_COLS], F32, name="bank%d" % i) for i in range(BANKS)]
-        turn = [0]
+        banks_used = [0]
 
-        def next_bank(among=BANKS):
-            turn[0] += 1
-            return banks[(turn[0] - 1) % among]
+        def next_bank():
+            banks_used[0] += 1
+            return banks[(banks_used[0] - 1) % BANKS]
 
-        def span_of(spans, col):
-            return [i for i, (c0, n) in enumerate(spans) if c0 <= col < c0 + n][0]
+        pairs = range(TASKS // PAIR)
+        g_slots = [(g, t) for g in range(OUT_PASSES) for t in range(PACK)]
+        halves = range(len(g_slots) // 2)
 
-        gt_pairs = [(g, t) for g in range(OUT_PASSES) for t in range(PACK)]
         ident = sb("ident", [P], F32)
         w_raw = sb("w_raw", [OUT_PASSES, PACK], BF16)
         w_pos = sb("w_pos", [OUT_PASSES * PACK], F32)
         w_neg = sb("w_neg", [OUT_PASSES * PACK], F32)
-        g_raw = {gt: sb("g_raw%d%d" % gt, [N_IN], BF16) for gt in gt_pairs}
-        g_stage = [sb("g_grp%d" % i, [2 * N_IN], BF16) for i in range(2)]
-        g_codes = [sb("g_codes%d" % i, [2 * IN_PASSES * P], U32) for i in range(PACK)]
-        g_scales = [sb("g_scales%d" % i, [2 * IN_PASSES * P], U8) for i in range(PACK)]
+        g_raw = {gt: sb("g_raw%d%d" % gt, [N_IN], BF16) for gt in g_slots}
+        g_grouped = [sb("g_grouped%d" % i, [2 * N_IN], BF16) for i in range(2)]
+        g_codes = [sb("g_codes%d" % h, [2 * IN_PASSES * P], U32) for h in halves]
+        g_scales = [sb("g_scales%d" % h, [2 * IN_PASSES * P], U8) for h in halves]
         l_raw = [sb("l_raw%d" % c, [OUT_PASSES, 2 * K_PASS], U8) for c in range(IN_PASSES)]
         l_words = [sb("l_words%d" % c, [OUT_PASSES, 2 * K_PASS], U8) for c in range(IN_PASSES)]
-        ls_raw = sb("ls_raw", [OUT_PASSES, N_IN], U8)
+        l_scales_raw = sb("l_scales_raw", [OUT_PASSES, N_IN], U8)
         l_scales = [sb("l_scales%d" % c, [OUT_PASSES, K_PASS], U8) for c in range(IN_PASSES)]
-        u_raw = {(s, c): sb("u_raw%d%d" % (s, c), [PACK, n], BF16) for s, (c0, n) in enumerate(LOAD_SPANS) for c in range(IN_PASSES)}
-        r_raw = {(s, g): sb("r_raw%d%d" % (s, g), [PACK, n], BF16) for s, (c0, n) in enumerate(LOAD_SPANS) for g in range(OUT_PASSES)}
-        pairs = range(TASKS // PAIR)
-        units = range(TASKS // UNIT)
-        u_grp = [sb("u_grp%d" % k, [IN_PASSES * PAIR * PACK], BF16) for k in pairs]
+        u_raw = {(s, c): sb("u_raw%d%d" % (s, c), [PACK, n], BF16) for s, (first, n) in enumerate(LOAD_SPANS) for c in range(IN_PASSES)}
+        r_raw = {(s, g): sb("r_raw%d%d" % (s, g), [PACK, n], BF16) for s, (first, n) in enumerate(LOAD_SPANS) for g in range(OUT_PASSES)}
+        u_grouped = [sb("u_grouped%d" % k, [IN_PASSES * PAIR * PACK], BF16) for k in pairs]
         u_codes = [sb("u_codes%d" % k, [IN_PASSES * PAIR], U32) for k in pairs]
         u_scales = [sb("u_scales%d" % k, [IN_PASSES * PAIR], U8) for k in pairs]
-        y_f32 = {(s, g): sb("y_f32%d%d" % (s, g), [PACK, n], F32) for s, (c0, n) in enumerate(LAST_SPANS) for g in range(OUT_PASSES)}
-        e_stage = [sb("e_grp%d" % j, [OUT_PASSES * UNIT * PACK], BF16) for j in range(4)]
-        e_grp = [e_stage[j % 4] for j in units]
-        e_codes = [sb("e_codes%d" % j, [OUT_PASSES * UNIT], U32) for j in units]
-        e_scales = [sb("e_scales%d" % j, [OUT_PASSES * UNIT], U8) for j in units]
-        u1_codes = [sb("u1_codes%d" % s, [IN_PASSES * n], U32) for s, (c0, n) in enumerate(LAST_SPANS)]
-        u1_scales = [sb("u1_scales%d" % s, [IN_PASSES * n], U8) for s, (c0, n) in enumerate(LAST_SPANS)]
-        y_stage = [sb("y_grp%d" % i, [PAIR * PACK], BF16) for i in range(4)]
-        y_grp = {(s, g): y_stage[(2 * s + g) % 4][:, : n * PACK] for s, (c0, n) in enumerate(LAST_SPANS) for g in range(OUT_PASSES)}
-        y_codes = [sb("y_codes%d" % s, [OUT_PASSES, n], U32) for s, (c0, n) in enumerate(LAST_SPANS)]
-        y_scales = [sb("y_scales%d" % i, [OUT_PASSES, n], U8) for i, (c0, n) in enumerate(SCALE_SPANS)]
+        y_f32 = {(s, g): sb("y_f32%d%d" % (s, g), [PACK, n], F32) for s, (first, n) in enumerate(Y_SPANS) for g in range(OUT_PASSES)}
+        e_grouped = [sb("e_grouped%d" % i, [OUT_PASSES * UNIT * PACK], BF16) for i in range(E_TILES)]
+        e_codes = [sb("e_codes%d" % i, [OUT_PASSES * UNIT], U32) for i in range(E_TILES)]
+        e_scales = [sb("e_scales%d" % i, [OUT_PASSES * UNIT], U8) for i in range(E_TILES)]
+        u1_codes = [sb("u1_codes%d" % i, [IN_PASSES * PAIR], U32) for i in range(U1_TILES)]
+        u1_scales = [sb("u1_scales%d" % i, [IN_PASSES * PAIR], U8) for i in range(U1_TILES)]
+        warm_in = sb("warm_in", [K_PASS], BF16)
+        warm_codes = sb("warm_codes", [P], U32)
+        warm_scales = sb("warm_scales", [P], U8)
+        y_grouped = [sb("y_grouped%d" % i, [PAIR * PACK], BF16) for i in range(Y_TILES)]
+        y_codes = {(k, g): sb("y_codes%d%d" % (k, g), [PAIR], U32) for k in pairs for g in range(OUT_PASSES)}
+        y_scales = [sb("y_scales%d" % i, [OUT_PASSES, n], U8) for i, (first, n) in enumerate(SCALE_SPANS)]
 
         def load_g(g, t):
             rows = plant[g * K_PASS : (g + 1) * K_PASS, :].rearrange("(m t) k -> m t k", t=PACK)
             nc.sync.dma_start(out=g_raw[g, t][:], in_=rows[:, t, :])
 
         def load_u(s, c):
-            c0, n = LOAD_SPANS[s]
-            rows = u[c * K_PASS : (c + 1) * K_PASS, c0 : c0 + n]
+            first, n = LOAD_SPANS[s]
+            rows = u[c * K_PASS : (c + 1) * K_PASS, first : first + n]
             nc.sync.dma_start(out=u_raw[s, c][:], in_=rows.rearrange("(p t) m -> p t m", t=PACK))
 
         def load_r(s, g):
-            c0, n = LOAD_SPANS[s]
-            rows = r[g * K_PASS : (g + 1) * K_PASS, c0 : c0 + n]
+            first, n = LOAD_SPANS[s]
+            rows = r[g * K_PASS : (g + 1) * K_PASS, first : first + n]
             nc.sync.dma_start(out=r_raw[s, g][:], in_=rows.rearrange("(p t) m -> p t m", t=PACK))
 
         def load_l(c):
             cols = learn_words[:, :, 2 * c * K_PASS : 2 * (c + 1) * K_PASS]
             nc.sync.dma_start(out=l_raw[c][:].bitcast(I32), in_=cols.rearrange("g p b -> p g b").bitcast(I32))
 
+        def load_l_scales():
+            for q in range(QUADRANTS):
+                nc.sync.dma_start(
+                    out=l_scales_raw[32 * q : 32 * q + 4, :, :].bitcast(I32),
+                    in_=learn_scales[:, 4 * q : 4 * q + 4, :].rearrange("g r n -> r g n").bitcast(I32),
+                )
+
         waiting = []
         chores = []
 
-        def defer(key, lag, fn):
-            waiting.append([key, lag, fn])
+        def defer(key, beats, call):
+            waiting.append([key, beats, call])
 
         def settle(key):
             for item in [x for x in waiting if x[0] == key]:
                 waiting.remove(item)
                 item[2]()
 
-        def tick(n_chores=1):
+        def beat():
             for item in list(waiting):
                 item[1] -= 1
                 if item[1] < 0:
                     waiting.remove(item)
                     item[2]()
-            for fn in chores[:n_chores]:
-                chores.remove(fn)
-                fn()
+            for call in chores[:1]:
+                chores.remove(call)
+                call()
 
         def quantize(codes, scales, grouped):
             nc.vector.quantize_mx(out=codes.bitcast(FP8X4), scales=scales, in_=grouped)
 
-        def interleaved(grouped):
+        def grouped_view(grouped):
             return grouped.rearrange("p (c i t) -> p c t i", i=4, t=PACK)
 
-        def by_four(rows):
+        def rows_view(rows):
             return rows.rearrange("p t (c i) -> p c t i", i=4)
 
-        def turn_g(i):
-            g, h = divmod(i, 2)
-            for b in range(3):
-                bank = next_bank(TURN_BANKS)
+        def warm(passes):
+            for i in range(passes):
+                nc.tensor.matmul_mx(
+                    out=banks[BANKS - 1][:, :P],
+                    lhsT=warm_codes[:].bitcast(FP8X4),
+                    lhsT_scale=warm_scales[:],
+                    rhs=warm_codes[:].bitcast(FP8X4),
+                    rhs_scale=warm_scales[:],
+                    start=True,
+                    stop=True,
+                )
+
+        def turn_g(h):
+            for b in range(IN_PASSES):
+                bank = banks[(IN_PASSES * h + b) % TURN_BANKS]
                 for x in range(2):
-                    t, c = divmod(2 * b + x, IN_PASSES)
-                    words = g_raw[g, 2 * h + t][:].bitcast(F32)
-                    for half in range(2):
-                        col = (x * 2 + half) * P
-                        nc.tensor.transpose(bank[:, col : col + P], words[:, c * 2 * P + half : (c + 1) * 2 * P : 2], ident[:])
-                dst = g_stage[h][:, b * 2 * K_PASS : (b + 1) * 2 * K_PASS].bitcast(F32)
+                    slot, c = divmod(2 * b + x, IN_PASSES)
+                    words = g_raw[g_slots[2 * h + slot]][:].bitcast(F32)
+                    for odd in range(2):
+                        col = (2 * x + odd) * P
+                        nc.tensor.transpose(bank[:, col : col + P], words[:, 2 * c * P + odd : 2 * (c + 1) * P : 2], ident[:])
+                dst = g_grouped[h % 2][:, b * 2 * K_PASS : (b + 1) * 2 * K_PASS].bitcast(F32)
                 nc.scalar.copy(out=dst.rearrange("p (x m v) -> p x m v", m=P, v=2), in_=bank[:].rearrange("p (x v m) -> p x m v", m=P, v=2))
 
-        def quantize_g(i, part):
-            b0, nb = PARTS[part]
-            cols = slice(b0 * 2 * P, (b0 + nb) * 2 * P)
-            quantize(g_codes[i][:, cols], g_scales[i][:, cols], g_stage[i % 2][:, b0 * 2 * K_PASS : (b0 + nb) * 2 * K_PASS])
-
-        def g_operand(g, t, c):
-            i = 2 * g + t // 2
-            cols = slice(((t % 2) * IN_PASSES + c) * P, ((t % 2) * IN_PASSES + c + 1) * P)
-            return g_codes[i][:, cols].bitcast(FP8X4), g_scales[i][:, cols]
+        def quantize_g(h, part):
+            first, count = PARTS[part]
+            cols = slice(first * 2 * P, (first + count) * 2 * P)
+            quantize(g_codes[h][:, cols], g_scales[h][:, cols], g_grouped[h % 2][:, first * 2 * K_PASS : (first + count) * 2 * K_PASS])
 
         def u_rows(k, c):
             s = span_of(LOAD_SPANS, k * PAIR)
             off = k * PAIR - LOAD_SPANS[s][0]
             return u_raw[s, c][:, :, off : off + PAIR]
 
-        def u_pass(k, c):
-            return u_grp[k][:, c * PAIR * PACK : (c + 1) * PAIR * PACK]
+        def r_rows(g, first, n):
+            s = span_of(LOAD_SPANS, first)
+            off = first - LOAD_SPANS[s][0]
+            return r_raw[s, g][:, :, off : off + n]
 
-        def group_u_vector(k, c):
-            nc.vector.tensor_copy(out=interleaved(u_pass(k, c)), in_=by_four(u_rows(k, c)))
+        def u_pass(k, c):
+            return u_grouped[k][:, c * PAIR * PACK : (c + 1) * PAIR * PACK]
+
+        def group_u_on_vector(k, c):
+            nc.vector.tensor_copy(out=grouped_view(u_pass(k, c)), in_=rows_view(u_rows(k, c)))
+
+        def group_u_on_scalar(k, c):
+            nc.scalar.copy(out=grouped_view(u_pass(k, c)), in_=rows_view(u_rows(k, c)))
 
         def quantize_u(k, part):
-            c0, n = PARTS[part]
-            cols = slice(c0 * PAIR, (c0 + n) * PAIR)
-            quantize(u_codes[k][:, cols], u_scales[k][:, cols], u_grp[k][:, c0 * PAIR * PACK : (c0 + n) * PAIR * PACK])
+            first, count = PARTS[part]
+            cols = slice(first * PAIR, (first + count) * PAIR)
+            quantize(u_codes[k][:, cols], u_scales[k][:, cols], u_grouped[k][:, first * PAIR * PACK : (first + count) * PAIR * PACK])
 
-        def group_u(k, c):
-            nc.scalar.copy(out=interleaved(u_pass(k, c)), in_=by_four(u_rows(k, c)))
+        def prepare_u(k, c):
+            group_u_on_scalar(k, c)
             if c > 0:
                 defer(("u", k), U_LAG, lambda: quantize_u(k, c - 1))
 
-        def r_rows(g, c0, n):
-            s = span_of(LOAD_SPANS, c0)
-            off = c0 - LOAD_SPANS[s][0]
-            return r_raw[s, g][:, :, off : off + n]
+        def order_l_words(c, g):
+            nc.vector.tensor_copy(
+                out=l_words[c][:, g, :].rearrange("p (t m b) -> p t m b", t=PACK, b=2),
+                in_=l_raw[c][:, g, :].rearrange("p (m t b) -> p t m b", t=PACK, b=2),
+            )
+
+        def order_l_scales(c):
+            nc.vector.tensor_copy(
+                out=l_scales[c][:].rearrange("p g (t m) -> p g t m", t=PACK),
+                in_=l_scales_raw[:, :, c * K_PASS : (c + 1) * K_PASS].rearrange("p g (m t) -> p g t m", t=PACK),
+            )
 
         def weigh(s, g, rows):
             for t in range(PACK):
                 col = g * PACK + t
                 nc.scalar.activation(out=y_f32[s, g][:, t, :], in_=rows[:, t, :], func=ACT.Copy, scale=w_pos[:, col : col + 1])
 
-        def order_l_words(c):
-            nc.vector.tensor_copy(
-                out=l_words[c][:].rearrange("p g (t m b) -> p g t m b", t=PACK, b=2),
-                in_=l_raw[c][:].rearrange("p g (m t b) -> p g t m b", t=PACK, b=2),
-            )
-
-        def order_l_scales(c):
-            nc.vector.tensor_copy(
-                out=l_scales[c][:].rearrange("p g (t m) -> p g t m", t=PACK),
-                in_=ls_raw[:, :, c * K_PASS : (c + 1) * K_PASS].rearrange("p g (m t) -> p g t m", t=PACK),
-            )
-
-        def error_now_sums(bank, j, g, t):
-            k, off = divmod(j * UNIT, PAIR)
+        def g_times(out, g, t, codes, scales, width, off):
+            n = out.shape[1]
             for c in range(IN_PASSES):
+                at = ((t % 2) * IN_PASSES + c) * P
                 nc.tensor.matmul_mx(
-                    out=bank[:, t * P : (t + 1) * P],
-                    lhsT=g_operand(g, t, c)[0],
-                    lhsT_scale=g_operand(g, t, c)[1],
-                    rhs=u_codes[k][:, c * PAIR + off : c * PAIR + off + UNIT].bitcast(FP8X4),
-                    rhs_scale=u_scales[k][:, c * PAIR + off : c * PAIR + off + UNIT],
+                    out=out,
+                    lhsT=g_codes[2 * g + t // 2][:, at : at + P].bitcast(FP8X4),
+                    lhsT_scale=g_scales[2 * g + t // 2][:, at : at + P],
+                    rhs=codes[:, c * width + off : c * width + off + n].bitcast(FP8X4),
+                    rhs_scale=scales[:, c * width + off : c * width + off + n],
                     start=(c == 0),
                     stop=(c == IN_PASSES - 1),
                 )
 
-        def error_now(j, g):
-            settle(("u", j * UNIT // PAIR))
-            bank = next_bank()
-            for t in range(PACK):
-                error_now_sums(bank, j, g, t)
-            error_now_out(bank, j, g)
+        def error_sums(bank, j, g, t):
+            k, off = divmod(j * UNIT, PAIR)
+            g_times(bank[:, t * P : (t + 1) * P], g, t, u_codes[k], u_scales[k], PAIR, off)
 
-        def error_now_out(bank, j, g):
+        def error_out(bank, j, g):
             nc.vector.tensor_tensor(
-                out=interleaved(e_grp[j][:, g * K_PASS : (g + 1) * K_PASS]),
-                in0=by_four(r_rows(g, j * UNIT, UNIT)),
-                in1=by_four(bank[:].rearrange("p (t m) -> p t m", t=PACK)),
+                out=grouped_view(e_grouped[j % E_TILES][:, g * K_PASS : (g + 1) * K_PASS]),
+                in0=rows_view(r_rows(g, j * UNIT, UNIT)),
+                in1=rows_view(bank[:].rearrange("p (t m) -> p t m", t=PACK)),
                 op=ALU.subtract,
             )
-            tick()
-            if g == OUT_PASSES - 1:
-                defer(("e", j), 0, lambda: quantize(e_codes[j][:], e_scales[j][:], e_grp[j][:]))
 
-        def learn(j, c):
+        def quantize_e(j):
+            quantize(e_codes[j % E_TILES][:], e_scales[j % E_TILES][:], e_grouped[j % E_TILES][:])
+
+        def error(j):
+            settle(("u", j * UNIT // PAIR))
+            for g in range(OUT_PASSES):
+                bank = next_bank()
+                for t in range(PACK):
+                    error_sums(bank, j, g, t)
+                error_out(bank, j, g)
+                beat()
+            defer(("e", j), 0, lambda: quantize_e(j))
+
+        def learn_pass(j, c):
             settle(("e", j))
-            settle(("l", c))
             bank = next_bank()
             for t in range(PACK):
                 for g in range(OUT_PASSES):
@@ -243,201 +272,189 @@ def tile_lifted_learning_control_error_k1_kernel(tc, u, r, plant, learn_words, l
                         out=bank[:, t * P : (t + 1) * P],
                         lhsT=l_words[c][:, g, 2 * t * P : 2 * (t + 1) * P].bitcast(FP4X4),
                         lhsT_scale=l_scales[c][:, g, t * P : (t + 1) * P],
-                        rhs=e_codes[j][:, g * UNIT : (g + 1) * UNIT].bitcast(FP8X4),
-                        rhs_scale=e_scales[j][:, g * UNIT : (g + 1) * UNIT],
+                        rhs=e_codes[j % E_TILES][:, g * UNIT : (g + 1) * UNIT].bitcast(FP8X4),
+                        rhs_scale=e_scales[j % E_TILES][:, g * UNIT : (g + 1) * UNIT],
                         start=(g == 0),
                         stop=(g == OUT_PASSES - 1),
                     )
             k, off = divmod(j * UNIT, PAIR)
-            s = span_of(LAST_SPANS, j * UNIT)
-            c0, n = LAST_SPANS[s]
-            soff = j * UNIT - c0
-            u_here = u_pass(k, c)[:, off * PACK : (off + UNIT) * PACK].rearrange("p (m t) -> p m t", t=PACK)
-            nc.vector.tensor_tensor(
-                out=u_here,
-                in0=u_here,
-                in1=bank[:].rearrange("p (t m) -> p m t", t=PACK),
-                op=ALU.add,
-            )
-            tick()
+            here = u_pass(k, c)[:, off * PACK : (off + UNIT) * PACK]
+            by_column = here.rearrange("p (m t) -> p m t", t=PACK)
+            nc.vector.tensor_tensor(out=by_column, in0=by_column, in1=bank[:].rearrange("p (t m) -> p m t", t=PACK), op=ALU.add)
+            beat()
+            s = span_of(Y_SPANS, j * UNIT)
+            n = Y_SPANS[s][1]
+            codes, scales = u1_codes[s % U1_TILES], u1_scales[s % U1_TILES]
             if n == UNIT:
-                src = u_pass(k, c)[:, off * PACK : (off + UNIT) * PACK]
-                defer(("u1", s), 0, lambda: quantize(u1_codes[s][:, c * n : (c + 1) * n], u1_scales[s][:, c * n : (c + 1) * n], src))
-            elif soff + UNIT == n and c > 0:
+                defer(("u1", s), 0, lambda: quantize(codes[:, c * n : (c + 1) * n], scales[:, c * n : (c + 1) * n], here))
+            elif off + UNIT == PAIR and c > 0:
                 first, count = PARTS[c - 1]
                 cols = slice(first * n, (first + count) * n)
-                src = u_grp[k][:, first * n * PACK : (first + count) * n * PACK]
-                defer(("u1", s), 0, lambda: quantize(u1_codes[s][:, cols], u1_scales[s][:, cols], src))
+                done = u_grouped[k][:, first * n * PACK : (first + count) * n * PACK]
+                defer(("u1", s), 0, lambda: quantize(codes[:, cols], scales[:, cols], done))
 
-        def store_y_scales(i):
-            c0, n = SCALE_SPANS[i]
-            for q in range(4):
-                engine = nc.scalar if q % 2 and c0 + n == TASKS else nc.sync
-                engine.dma_start(
-                    out=out_2[:, 4 * q : 4 * q + 4, c0 : c0 + n].rearrange("g r n -> r g n").bitcast(I32),
-                    in_=y_scales[i][32 * q : 32 * q + 4, :, :].bitcast(I32),
-                )
+        def learn(j):
+            for c in range(IN_PASSES):
+                learn_pass(j, c)
+
+        def y_grouped_of(s, g):
+            return y_grouped[(OUT_PASSES * s + g) % Y_TILES][:, : Y_SPANS[s][1] * PACK]
 
         def quantize_y(s, g):
-            c0, n = LAST_SPANS[s]
-            i = span_of(SCALE_SPANS, c0)
-            off = c0 - SCALE_SPANS[i][0]
-            quantize(y_codes[s][:, g, :], y_scales[i][:, g, off : off + n], y_grp[s, g])
-            dst = out_1[g, :, c0 : c0 + n, :].rearrange("p m t -> p (m t)")
-            nc.sync.dma_start(out=dst.bitcast(I32), in_=y_codes[s][:, g, :].bitcast(I32))
-            if g == OUT_PASSES - 1 and off + n == SCALE_SPANS[i][1]:
-                store_y_scales(i)
+            first, n = Y_SPANS[s]
+            i = span_of(SCALE_SPANS, first)
+            scale_first, scale_n = SCALE_SPANS[i]
+            k, off = divmod(first, PAIR)
+            quantize(y_codes[k, g][:, off : off + n], y_scales[i][:, g, first - scale_first : first - scale_first + n], y_grouped_of(s, g))
+            queue = nc.scalar if first + n == TASKS and g == OUT_PASSES - 1 else nc.sync
+            if off + n == PAIR:
+                dst = out_1[g, :, k * PAIR : (k + 1) * PAIR, :].rearrange("p m t -> p (m t)")
+                queue.dma_start(out=dst.bitcast(I32), in_=y_codes[k, g][:].bitcast(I32))
+            if g == OUT_PASSES - 1 and first + n == scale_first + scale_n:
+                for q in range(QUADRANTS):
+                    queue.dma_start(
+                        out=out_2[:, 4 * q : 4 * q + 4, scale_first : scale_first + scale_n].rearrange("g r n -> r g n").bitcast(I32),
+                        in_=y_scales[i][32 * q : 32 * q + 4, :, :].bitcast(I32),
+                    )
 
-        def error_next(s, g):
-            settle(("u1", s))
-            c0, n = LAST_SPANS[s]
+        def next_error_group(s, g):
+            first, n = Y_SPANS[s]
+            y = y_f32[s, g]
             per_bank = BANK_COLS // n
             for t0 in range(0, PACK, per_bank):
                 bank = next_bank()
                 for i in range(per_bank):
-                    t = t0 + i
-                    for c in range(IN_PASSES):
-                        nc.tensor.matmul_mx(
-                            out=bank[:, i * n : (i + 1) * n],
-                            lhsT=g_operand(g, t, c)[0],
-                            lhsT_scale=g_operand(g, t, c)[1],
-                            rhs=u1_codes[s][:, c * n : (c + 1) * n].bitcast(FP8X4),
-                            rhs_scale=u1_scales[s][:, c * n : (c + 1) * n],
-                            start=(c == 0),
-                            stop=(c == IN_PASSES - 1),
-                        )
-                if s in FUSED:
-                    for i in range(per_bank):
-                        t = t0 + i
+                    g_times(bank[:, i * n : (i + 1) * n], g, t0 + i, u1_codes[s % U1_TILES], u1_scales[s % U1_TILES], n, 0)
+                if n == UNIT:
+                    for t in range(PACK):
                         col = g * PACK + t
                         nc.vector.scalar_tensor_tensor(
-                            out=y_f32[s, g][:, t, :],
-                            in0=bank[:, i * n : (i + 1) * n],
+                            out=y[:, t, :],
+                            in0=bank[:, t * n : (t + 1) * n],
                             scalar=w_neg[:, col : col + 1],
-                            in1=y_f32[s, g][:, t, :],
+                            in1=y[:, t, :],
                             op0=ALU.mult,
                             op1=ALU.add,
                         )
+                        if t == 0:
+                            beat()
                 else:
                     nc.vector.tensor_tensor(
-                        out=y_f32[s, g][:, t0 : t0 + per_bank, :],
-                        in0=r_rows(g, c0, n)[:, t0 : t0 + per_bank, :],
+                        out=y[:, t0 : t0 + per_bank, :],
+                        in0=r_rows(g, first, n)[:, t0 : t0 + per_bank, :],
                         in1=bank[:].rearrange("p (t m) -> p t m", t=per_bank),
                         op=ALU.subtract,
                     )
+                    if t0 + per_bank == PACK:
+                        weigh(s, g, y)
                 if t0 + per_bank == PACK:
-                    if s not in FUSED:
-                        weigh(s, g, y_f32[s, g])
-                    y_rows = y_f32[s, g][:]
-                    nc.scalar.copy(out=interleaved(y_grp[s, g]), in_=by_four(y_rows))
-                    dst = out_0[g * K_PASS : (g + 1) * K_PASS, c0 : c0 + n].rearrange("(p t) m -> p t m", t=PACK)
-                    nc.sync.dma_start(out=dst, in_=y_rows)
-                tick()
-            defer(("y", s, g), Y_LAG, lambda: quantize_y(s, g))
+                    dst = out_0[g * K_PASS : (g + 1) * K_PASS, first : first + n].rearrange("(p t) m -> p t m", t=PACK)
+                    nc.sync.dma_start(out=dst, in_=y[:])
+                if n != UNIT:
+                    beat()
+            nc.scalar.copy(out=grouped_view(y_grouped_of(s, g)), in_=rows_view(y[:]))
+            defer(("y", s, g), Y_LAG_NARROW if n == UNIT else Y_LAG_WIDE, lambda: quantize_y(s, g))
+
+        def next_error(s):
+            settle(("u1", s))
+            for g in range(OUT_PASSES):
+                next_error_group(s, g)
 
         make_identity(nc, ident[:])
-        nc.vector.memset(ls_raw[:].rearrange("p g n -> p (g n)").bitcast(I32), 0)
+        nc.vector.memset(l_scales_raw[:].rearrange("p g n -> p (g n)").bitcast(I32), 0)
+        nc.vector.memset(warm_in[:], 1.0)
+        quantize(warm_codes[:], warm_scales[:], warm_in[:])
         nc.scalar.dma_start(out=w_raw[:], in_=w.rearrange("(g p t) o -> p g (t o)", g=OUT_PASSES, t=PACK))
-        for q in range(4):
-            nc.scalar.dma_start(
-                out=ls_raw[32 * q : 32 * q + 4, :, :].bitcast(I32),
-                in_=learn_scales[:, 4 * q : 4 * q + 4, :].rearrange("g r n -> r g n").bitcast(I32),
-            )
-        load_u(0, 0)
-        load_u(0, 1)
-        load_u(0, 2)
         load_g(0, 0)
-        load_g(0, 1)
+        load_l_scales()
         load_l(0)
-        load_g(0, 2)
-        load_g(0, 3)
-        load_r(0, 0)
+        for t in range(1, PACK):
+            load_g(0, t)
+        for c in range(IN_PASSES):
+            load_u(0, c)
         load_g(1, 0)
         load_g(1, 1)
         load_l(1)
         load_g(1, 2)
         load_g(1, 3)
-        load_r(0, 1)
+        for g in range(OUT_PASSES):
+            load_r(0, g)
         load_l(2)
-        load_u(1, 0)
-        load_u(1, 1)
-        load_u(1, 2)
-        load_r(1, 0)
-        load_r(1, 1)
-        load_u(2, 0)
-        load_u(2, 1)
-        load_u(2, 2)
-        load_r(2, 0)
-        load_r(2, 1)
-
+        for s in range(1, len(LOAD_SPANS)):
+            for c in range(IN_PASSES):
+                load_u(s, c)
+            for g in range(OUT_PASSES):
+                load_r(s, g)
         w_flat = w_raw[:].rearrange("p g t -> p (g t)")
         nc.scalar.activation(out=w_pos[:], in_=w_flat, func=ACT.Copy, scale=1.0)
         nc.scalar.activation(out=w_neg[:], in_=w_flat, func=ACT.Copy, scale=-1.0)
 
-        def first_sums(i):
-            settle(("u", 0))
-            g, t = gt_pairs[i]
-            for j in range(2):
-                error_now_sums(banks[TURN_BANKS + 2 * g + j], j, g, t)
+        def first_bank(j, g):
+            return banks[TURN_BANKS + 2 * g + j]
 
-        order_l_scales(0)
-        order_l_scales(1)
-        order_l_scales(2)
+        def first_sums(g, slots):
+            for j in range(2):
+                for t in slots:
+                    error_sums(first_bank(j, g), j, g, t)
+
+        warm(WARM_FIRST)
+        order_l_words(0, 0)
+        order_l_words(0, 1)
         turn_g(0)
-        group_u(0, 0)
-        group_u_vector(0, 1)
-        quantize_u(0, 0)
-        group_u_vector(0, 2)
-        quantize_u(0, 1)
-        quantize_g(0, 0)
-        quantize_g(0, 1)
+        order_l_scales(0)
         turn_g(1)
-        settle(("u", 0))
-        first_sums(0)
-        first_sums(1)
+        warm(WARM_SECOND)
+        quantize_g(0, 0)
+        group_u_on_scalar(0, 0)
+        group_u_on_vector(0, 1)
+        quantize_g(0, 1)
+        group_u_on_vector(0, 2)
         quantize_g(1, 0)
-        quantize_g(1, 1)
+        quantize_u(0, 0)
+        quantize_u(0, 1)
         turn_g(2)
-        first_sums(2)
-        first_sums(3)
+        quantize_g(1, 1)
+        order_l_scales(1)
+        for t in range(PACK):
+            first_sums(0, [t])
+        order_l_words(1, 0)
+        order_l_words(1, 1)
+        turn_g(3)
         quantize_g(2, 0)
         quantize_g(2, 1)
-        order_l_words(0)
-        turn_g(3)
-        error_now_out(banks[TURN_BANKS + 2 * 0 + 0], 0, 0)
-        error_now_out(banks[TURN_BANKS + 2 * 0 + 1], 1, 0)
-        first_sums(4)
-        first_sums(5)
+        order_l_scales(2)
+        error_out(first_bank(0, 0), 0, 0)
+        first_sums(1, [0, 1])
+        error_out(first_bank(1, 0), 1, 0)
         quantize_g(3, 0)
         quantize_g(3, 1)
-        first_sums(6)
-        first_sums(7)
-        group_u(1, 0)
-        group_u(1, 1)
-        group_u(1, 2)
-        error_now_out(banks[TURN_BANKS + 2 * 1 + 0], 0, 1)
-        error_now_out(banks[TURN_BANKS + 2 * 1 + 1], 1, 1)
-        defer(("l", 1), 1, lambda: order_l_words(1))
-        defer(("l", 2), 2, lambda: order_l_words(2))
-        for k in range(2, len(pairs)):
-            chores.extend([lambda k=k, c=c: group_u(k, c) for c in range(IN_PASSES)])
-        for s in FUSED:
-            chores.extend([lambda s=s, g=g: weigh(s, g, r_rows(g, *LAST_SPANS[s])) for g in range(OUT_PASSES)])
-        turn[0] = 0
+        for c in range(IN_PASSES):
+            group_u_on_scalar(1, c)
+        order_l_words(2, 0)
+        first_sums(1, [2, 3])
+        order_l_words(2, 1)
+        for j in range(2):
+            error_out(first_bank(j, 1), j, 1)
+            quantize_e(j)
+        learn_pass(0, 0)
+        quantize_u(1, 0)
+        learn_pass(0, 1)
+        quantize_u(1, 1)
+        learn_pass(0, 2)
+        learn(1)
 
-        def stage1(j):
-            for g in range(OUT_PASSES):
-                error_now(j, g)
-
-        def stage2(j):
-            for c in range(IN_PASSES):
-                learn(j, c)
-
-        def stage3(s):
-            for g in range(OUT_PASSES):
-                error_next(s, g)
-
-        for step, i in ORDER:
-            [stage1, stage2, stage3][step - 1](i)
+        for k in pairs[2:]:
+            chores.extend([lambda k=k, c=c: prepare_u(k, c) for c in range(IN_PASSES)])
+        for s, span in enumerate(Y_SPANS):
+            if span[1] == UNIT:
+                chores.extend([lambda s=s, g=g: weigh(s, g, r_rows(g, *Y_SPANS[s])) for g in range(OUT_PASSES)])
+        for k in pairs[1:]:
+            error(2 * k)
+            error(2 * k + 1)
+            next_error(k - 1)
+            learn(2 * k)
+            learn(2 * k + 1)
+        for s in range(len(pairs) - 1, len(Y_SPANS)):
+            next_error(s)
         for item in list(waiting):
-            item[2]()
+            settle(item[0])

from contextlib import ExitStack

import concourse.mybir as mybir
from concourse.masks import make_identity

N_IN, N_OUT, TASKS = 1536, 1024, 1024
FLOPS = 3 * 2 * N_IN * N_OUT * TASKS

F32 = mybir.dt.float32
BF16 = mybir.dt.bfloat16
I32 = mybir.dt.int32
U32 = mybir.dt.uint32
U8 = mybir.dt.uint8
FP8X4 = mybir.dt.float8_e4m3fn_x4
FP4X4 = mybir.dt.float4_e2m1fn_x4
ALU = mybir.AluOpType
ACT = mybir.ActivationFunctionType

P = 128
PACK = 4
K_PASS = P * PACK
IN_PASSES = N_IN // K_PASS
OUT_PASSES = N_OUT // K_PASS
QUADRANTS = 4
BANKS = 8
BANK_COLS = 512
TURN_BANKS = 4

UNIT = 128
PAIR = 2 * UNIT
LOAD_SPANS = [(0, 256), (256, 256), (512, 512)]
Y_SPANS = [(0, 256), (256, 256), (512, 256), (768, 128), (896, 128)]
SCALE_SPANS = [(0, 512), (512, 512)]
PARTS = [(0, 2), (2, 1)]

U_LAG = 3
Y_LAG_WIDE = 7
Y_LAG_NARROW = 3
E_TILES, U1_TILES, Y_TILES = 4, 3, 4
WARM_FIRST, WARM_SECOND = 10, 16


def tile_lifted_learning_control_error_k1_kernel(tc, u, r, plant, learn_words, learn_scales, w, out_0, out_1, out_2):
    nc = tc.nc
    with ExitStack() as ctx:
        keep = ctx.enter_context(tc.tile_pool(name="keep", bufs=1))
        psum = ctx.enter_context(tc.psum_pool(name="psum", bufs=1))
        ctx.enter_context(tc.manual_schedule())

        def sb(name, shape, dtype):
            return keep.tile([P] + shape, dtype, name=name, align_bytes=64)

        def span_of(spans, task):
            return [i for i, (first, count) in enumerate(spans) if first <= task < first + count][0]

        banks = [psum.tile([P, BANK_COLS], F32, name="bank%d" % i) for i in range(BANKS)]
        banks_used = [0]

        def next_bank():
            banks_used[0] += 1
            return banks[(banks_used[0] - 1) % BANKS]

        pairs = range(TASKS // PAIR)
        g_slots = [(g, t) for g in range(OUT_PASSES) for t in range(PACK)]
        halves = range(len(g_slots) // 2)

        ident = sb("ident", [P], F32)
        w_raw = sb("w_raw", [OUT_PASSES, PACK], BF16)
        w_pos = sb("w_pos", [OUT_PASSES * PACK], F32)
        w_neg = sb("w_neg", [OUT_PASSES * PACK], F32)
        g_raw = {gt: sb("g_raw%d%d" % gt, [N_IN], BF16) for gt in g_slots}
        g_grouped = [sb("g_grouped%d" % i, [2 * N_IN], BF16) for i in range(2)]
        g_codes = [sb("g_codes%d" % h, [2 * IN_PASSES * P], U32) for h in halves]
        g_scales = [sb("g_scales%d" % h, [2 * IN_PASSES * P], U8) for h in halves]
        l_raw = [sb("l_raw%d" % c, [OUT_PASSES, 2 * K_PASS], U8) for c in range(IN_PASSES)]
        l_words = [sb("l_words%d" % c, [OUT_PASSES, 2 * K_PASS], U8) for c in range(IN_PASSES)]
        l_scales_raw = sb("l_scales_raw", [OUT_PASSES, N_IN], U8)
        l_scales = [sb("l_scales%d" % c, [OUT_PASSES, K_PASS], U8) for c in range(IN_PASSES)]
        u_raw = {(s, c): sb("u_raw%d%d" % (s, c), [PACK, n], BF16) for s, (first, n) in enumerate(LOAD_SPANS) for c in range(IN_PASSES)}
        r_raw = {(s, g): sb("r_raw%d%d" % (s, g), [PACK, n], BF16) for s, (first, n) in enumerate(LOAD_SPANS) for g in range(OUT_PASSES)}
        u_grouped = [sb("u_grouped%d" % k, [IN_PASSES * PAIR * PACK], BF16) for k in pairs]
        u_codes = [sb("u_codes%d" % k, [IN_PASSES * PAIR], U32) for k in pairs]
        u_scales = [sb("u_scales%d" % k, [IN_PASSES * PAIR], U8) for k in pairs]
        y_f32 = {(s, g): sb("y_f32%d%d" % (s, g), [PACK, n], F32) for s, (first, n) in enumerate(Y_SPANS) for g in range(OUT_PASSES)}
        e_grouped = [sb("e_grouped%d" % i, [OUT_PASSES * UNIT * PACK], BF16) for i in range(E_TILES)]
        e_codes = [sb("e_codes%d" % i, [OUT_PASSES * UNIT], U32) for i in range(E_TILES)]
        e_scales = [sb("e_scales%d" % i, [OUT_PASSES * UNIT], U8) for i in range(E_TILES)]
        u1_codes = [sb("u1_codes%d" % i, [IN_PASSES * PAIR], U32) for i in range(U1_TILES)]
        u1_scales = [sb("u1_scales%d" % i, [IN_PASSES * PAIR], U8) for i in range(U1_TILES)]
        warm_in = sb("warm_in", [K_PASS], BF16)
        warm_codes = sb("warm_codes", [P], U32)
        warm_scales = sb("warm_scales", [P], U8)
        y_grouped = [sb("y_grouped%d" % i, [PAIR * PACK], BF16) for i in range(Y_TILES)]
        y_codes = {(k, g): sb("y_codes%d%d" % (k, g), [PAIR], U32) for k in pairs for g in range(OUT_PASSES)}
        y_scales = [sb("y_scales%d" % i, [OUT_PASSES, n], U8) for i, (first, n) in enumerate(SCALE_SPANS)]

        def load_g(g, t):
            rows = plant[g * K_PASS : (g + 1) * K_PASS, :].rearrange("(m t) k -> m t k", t=PACK)
            nc.sync.dma_start(out=g_raw[g, t][:], in_=rows[:, t, :])

        def load_u(s, c):
            first, n = LOAD_SPANS[s]
            rows = u[c * K_PASS : (c + 1) * K_PASS, first : first + n]
            nc.sync.dma_start(out=u_raw[s, c][:], in_=rows.rearrange("(p t) m -> p t m", t=PACK))

        def load_r(s, g):
            first, n = LOAD_SPANS[s]
            rows = r[g * K_PASS : (g + 1) * K_PASS, first : first + n]
            nc.sync.dma_start(out=r_raw[s, g][:], in_=rows.rearrange("(p t) m -> p t m", t=PACK))

        def load_l(c):
            cols = learn_words[:, :, 2 * c * K_PASS : 2 * (c + 1) * K_PASS]
            nc.sync.dma_start(out=l_raw[c][:].bitcast(I32), in_=cols.rearrange("g p b -> p g b").bitcast(I32))

        def load_l_scales():
            for q in range(QUADRANTS):
                nc.sync.dma_start(
                    out=l_scales_raw[32 * q : 32 * q + 4, :, :].bitcast(I32),
                    in_=learn_scales[:, 4 * q : 4 * q + 4, :].rearrange("g r n -> r g n").bitcast(I32),
                )

        waiting = []
        chores = []

        def defer(key, beats, call):
            waiting.append([key, beats, call])

        def settle(key):
            for item in [x for x in waiting if x[0] == key]:
                waiting.remove(item)
                item[2]()

        def beat():
            for item in list(waiting):
                item[1] -= 1
                if item[1] < 0:
                    waiting.remove(item)
                    item[2]()
            for call in chores[:1]:
                chores.remove(call)
                call()

        def quantize(codes, scales, grouped):
            nc.vector.quantize_mx(out=codes.bitcast(FP8X4), scales=scales, in_=grouped)

        def grouped_view(grouped):
            return grouped.rearrange("p (c i t) -> p c t i", i=4, t=PACK)

        def rows_view(rows):
            return rows.rearrange("p t (c i) -> p c t i", i=4)

        def warm(passes):
            for i in range(passes):
                nc.tensor.matmul_mx(
                    out=banks[BANKS - 1][:, :P],
                    lhsT=warm_codes[:].bitcast(FP8X4),
                    lhsT_scale=warm_scales[:],
                    rhs=warm_codes[:].bitcast(FP8X4),
                    rhs_scale=warm_scales[:],
                    start=True,
                    stop=True,
                )

        def turn_g(h):
            for b in range(IN_PASSES):
                bank = banks[(IN_PASSES * h + b) % TURN_BANKS]
                for x in range(2):
                    slot, c = divmod(2 * b + x, IN_PASSES)
                    words = g_raw[g_slots[2 * h + slot]][:].bitcast(F32)
                    for odd in range(2):
                        col = (2 * x + odd) * P
                        nc.tensor.transpose(bank[:, col : col + P], words[:, 2 * c * P + odd : 2 * (c + 1) * P : 2], ident[:])
                dst = g_grouped[h % 2][:, b * 2 * K_PASS : (b + 1) * 2 * K_PASS].bitcast(F32)
                nc.scalar.copy(out=dst.rearrange("p (x m v) -> p x m v", m=P, v=2), in_=bank[:].rearrange("p (x v m) -> p x m v", m=P, v=2))

        def quantize_g(h, part):
            first, count = PARTS[part]
            cols = slice(first * 2 * P, (first + count) * 2 * P)
            quantize(g_codes[h][:, cols], g_scales[h][:, cols], g_grouped[h % 2][:, first * 2 * K_PASS : (first + count) * 2 * K_PASS])

        def u_rows(k, c):
            s = span_of(LOAD_SPANS, k * PAIR)
            off = k * PAIR - LOAD_SPANS[s][0]
            return u_raw[s, c][:, :, off : off + PAIR]

        def r_rows(g, first, n):
            s = span_of(LOAD_SPANS, first)
            off = first - LOAD_SPANS[s][0]
            return r_raw[s, g][:, :, off : off + n]

        def u_pass(k, c):
            return u_grouped[k][:, c * PAIR * PACK : (c + 1) * PAIR * PACK]

        def group_u_on_vector(k, c):
            nc.vector.tensor_copy(out=grouped_view(u_pass(k, c)), in_=rows_view(u_rows(k, c)))

        def group_u_on_scalar(k, c):
            nc.scalar.copy(out=grouped_view(u_pass(k, c)), in_=rows_view(u_rows(k, c)))

        def quantize_u(k, part):
            first, count = PARTS[part]
            cols = slice(first * PAIR, (first + count) * PAIR)
            quantize(u_codes[k][:, cols], u_scales[k][:, cols], u_grouped[k][:, first * PAIR * PACK : (first + count) * PAIR * PACK])

        def prepare_u(k, c):
            group_u_on_scalar(k, c)
            if c > 0:
                defer(("u", k), U_LAG, lambda: quantize_u(k, c - 1))

        def order_l_words(c, g):
            nc.vector.tensor_copy(
                out=l_words[c][:, g, :].rearrange("p (t m b) -> p t m b", t=PACK, b=2),
                in_=l_raw[c][:, g, :].rearrange("p (m t b) -> p t m b", t=PACK, b=2),
            )

        def order_l_scales(c):
            nc.vector.tensor_copy(
                out=l_scales[c][:].rearrange("p g (t m) -> p g t m", t=PACK),
                in_=l_scales_raw[:, :, c * K_PASS : (c + 1) * K_PASS].rearrange("p g (m t) -> p g t m", t=PACK),
            )

        def weigh(s, g, rows):
            for t in range(PACK):
                col = g * PACK + t
                nc.scalar.activation(out=y_f32[s, g][:, t, :], in_=rows[:, t, :], func=ACT.Copy, scale=w_pos[:, col : col + 1])

        def g_times(out, g, t, codes, scales, width, off):
            n = out.shape[1]
            for c in range(IN_PASSES):
                at = ((t % 2) * IN_PASSES + c) * P
                nc.tensor.matmul_mx(
                    out=out,
                    lhsT=g_codes[2 * g + t // 2][:, at : at + P].bitcast(FP8X4),
                    lhsT_scale=g_scales[2 * g + t // 2][:, at : at + P],
                    rhs=codes[:, c * width + off : c * width + off + n].bitcast(FP8X4),
                    rhs_scale=scales[:, c * width + off : c * width + off + n],
                    start=(c == 0),
                    stop=(c == IN_PASSES - 1),
                )

        def error_sums(bank, j, g, t):
            k, off = divmod(j * UNIT, PAIR)
            g_times(bank[:, t * P : (t + 1) * P], g, t, u_codes[k], u_scales[k], PAIR, off)

        def error_out(bank, j, g):
            nc.vector.tensor_tensor(
                out=grouped_view(e_grouped[j % E_TILES][:, g * K_PASS : (g + 1) * K_PASS]),
                in0=rows_view(r_rows(g, j * UNIT, UNIT)),
                in1=rows_view(bank[:].rearrange("p (t m) -> p t m", t=PACK)),
                op=ALU.subtract,
            )

        def quantize_e(j):
            quantize(e_codes[j % E_TILES][:], e_scales[j % E_TILES][:], e_grouped[j % E_TILES][:])

        def error(j):
            settle(("u", j * UNIT // PAIR))
            for g in range(OUT_PASSES):
                bank = next_bank()
                for t in range(PACK):
                    error_sums(bank, j, g, t)
                error_out(bank, j, g)
                beat()
            defer(("e", j), 0, lambda: quantize_e(j))

        def learn_pass(j, c):
            settle(("e", j))
            bank = next_bank()
            for t in range(PACK):
                for g in range(OUT_PASSES):
                    nc.tensor.matmul_mx(
                        out=bank[:, t * P : (t + 1) * P],
                        lhsT=l_words[c][:, g, 2 * t * P : 2 * (t + 1) * P].bitcast(FP4X4),
                        lhsT_scale=l_scales[c][:, g, t * P : (t + 1) * P],
                        rhs=e_codes[j % E_TILES][:, g * UNIT : (g + 1) * UNIT].bitcast(FP8X4),
                        rhs_scale=e_scales[j % E_TILES][:, g * UNIT : (g + 1) * UNIT],
                        start=(g == 0),
                        stop=(g == OUT_PASSES - 1),
                    )
            k, off = divmod(j * UNIT, PAIR)
            here = u_pass(k, c)[:, off * PACK : (off + UNIT) * PACK]
            by_column = here.rearrange("p (m t) -> p m t", t=PACK)
            nc.vector.tensor_tensor(out=by_column, in0=by_column, in1=bank[:].rearrange("p (t m) -> p m t", t=PACK), op=ALU.add)
            beat()
            s = span_of(Y_SPANS, j * UNIT)
            n = Y_SPANS[s][1]
            codes, scales = u1_codes[s % U1_TILES], u1_scales[s % U1_TILES]
            if n == UNIT:
                defer(("u1", s), 0, lambda: quantize(codes[:, c * n : (c + 1) * n], scales[:, c * n : (c + 1) * n], here))
            elif off + UNIT == PAIR and c > 0:
                first, count = PARTS[c - 1]
                cols = slice(first * n, (first + count) * n)
                done = u_grouped[k][:, first * n * PACK : (first + count) * n * PACK]
                defer(("u1", s), 0, lambda: quantize(codes[:, cols], scales[:, cols], done))

        def learn(j):
            for c in range(IN_PASSES):
                learn_pass(j, c)

        def y_grouped_of(s, g):
            return y_grouped[(OUT_PASSES * s + g) % Y_TILES][:, : Y_SPANS[s][1] * PACK]

        def quantize_y(s, g):
            first, n = Y_SPANS[s]
            i = span_of(SCALE_SPANS, first)
            scale_first, scale_n = SCALE_SPANS[i]
            k, off = divmod(first, PAIR)
            quantize(y_codes[k, g][:, off : off + n], y_scales[i][:, g, first - scale_first : first - scale_first + n], y_grouped_of(s, g))
            queue = nc.scalar if first + n == TASKS and g == OUT_PASSES - 1 else nc.sync
            if off + n == PAIR:
                dst = out_1[g, :, k * PAIR : (k + 1) * PAIR, :].rearrange("p m t -> p (m t)")
                queue.dma_start(out=dst.bitcast(I32), in_=y_codes[k, g][:].bitcast(I32))
            if g == OUT_PASSES - 1 and first + n == scale_first + scale_n:
                for q in range(QUADRANTS):
                    queue.dma_start(
                        out=out_2[:, 4 * q : 4 * q + 4, scale_first : scale_first + scale_n].rearrange("g r n -> r g n").bitcast(I32),
                        in_=y_scales[i][32 * q : 32 * q + 4, :, :].bitcast(I32),
                    )

        def next_error_group(s, g):
            first, n = Y_SPANS[s]
            y = y_f32[s, g]
            per_bank = BANK_COLS // n
            for t0 in range(0, PACK, per_bank):
                bank = next_bank()
                for i in range(per_bank):
                    g_times(bank[:, i * n : (i + 1) * n], g, t0 + i, u1_codes[s % U1_TILES], u1_scales[s % U1_TILES], n, 0)
                if n == UNIT:
                    for t in range(PACK):
                        col = g * PACK + t
                        nc.vector.scalar_tensor_tensor(
                            out=y[:, t, :],
                            in0=bank[:, t * n : (t + 1) * n],
                            scalar=w_neg[:, col : col + 1],
                            in1=y[:, t, :],
                            op0=ALU.mult,
                            op1=ALU.add,
                        )
                        if t == 0:
                            beat()
                else:
                    nc.vector.tensor_tensor(
                        out=y[:, t0 : t0 + per_bank, :],
                        in0=r_rows(g, first, n)[:, t0 : t0 + per_bank, :],
                        in1=bank[:].rearrange("p (t m) -> p t m", t=per_bank),
                        op=ALU.subtract,
                    )
                    if t0 + per_bank == PACK:
                        weigh(s, g, y)
                if t0 + per_bank == PACK:
                    dst = out_0[g * K_PASS : (g + 1) * K_PASS, first : first + n].rearrange("(p t) m -> p t m", t=PACK)
                    nc.sync.dma_start(out=dst, in_=y[:])
                if n != UNIT:
                    beat()
            nc.scalar.copy(out=grouped_view(y_grouped_of(s, g)), in_=rows_view(y[:]))
            defer(("y", s, g), Y_LAG_NARROW if n == UNIT else Y_LAG_WIDE, lambda: quantize_y(s, g))

        def next_error(s):
            settle(("u1", s))
            for g in range(OUT_PASSES):
                next_error_group(s, g)

        make_identity(nc, ident[:])
        nc.vector.memset(l_scales_raw[:].rearrange("p g n -> p (g n)").bitcast(I32), 0)
        nc.vector.memset(warm_in[:], 1.0)
        quantize(warm_codes[:], warm_scales[:], warm_in[:])
        nc.scalar.dma_start(out=w_raw[:], in_=w.rearrange("(g p t) o -> p g (t o)", g=OUT_PASSES, t=PACK))
        load_g(0, 0)
        load_l_scales()
        load_l(0)
        for t in range(1, PACK):
            load_g(0, t)
        for c in range(IN_PASSES):
            load_u(0, c)
        load_g(1, 0)
        load_g(1, 1)
        load_l(1)
        load_g(1, 2)
        load_g(1, 3)
        for g in range(OUT_PASSES):
            load_r(0, g)
        load_l(2)
        for s in range(1, len(LOAD_SPANS)):
            for c in range(IN_PASSES):
                load_u(s, c)
            for g in range(OUT_PASSES):
                load_r(s, g)
        w_flat = w_raw[:].rearrange("p g t -> p (g t)")
        nc.scalar.activation(out=w_pos[:], in_=w_flat, func=ACT.Copy, scale=1.0)
        nc.scalar.activation(out=w_neg[:], in_=w_flat, func=ACT.Copy, scale=-1.0)

        def first_bank(j, g):
            return banks[TURN_BANKS + 2 * g + j]

        def first_sums(g, slots):
            for j in range(2):
                for t in slots:
                    error_sums(first_bank(j, g), j, g, t)

        warm(WARM_FIRST)
        order_l_words(0, 0)
        order_l_words(0, 1)
        turn_g(0)
        order_l_scales(0)
        turn_g(1)
        warm(WARM_SECOND)
        quantize_g(0, 0)
        group_u_on_scalar(0, 0)
        group_u_on_vector(0, 1)
        quantize_g(0, 1)
        group_u_on_vector(0, 2)
        quantize_g(1, 0)
        quantize_u(0, 0)
        quantize_u(0, 1)
        turn_g(2)
        quantize_g(1, 1)
        order_l_scales(1)
        for t in range(PACK):
            first_sums(0, [t])
        order_l_words(1, 0)
        order_l_words(1, 1)
        turn_g(3)
        quantize_g(2, 0)
        quantize_g(2, 1)
        order_l_scales(2)
        error_out(first_bank(0, 0), 0, 0)
        first_sums(1, [0, 1])
        error_out(first_bank(1, 0), 1, 0)
        quantize_g(3, 0)
        quantize_g(3, 1)
        for c in range(IN_PASSES):
            group_u_on_scalar(1, c)
        order_l_words(2, 0)
        first_sums(1, [2, 3])
        order_l_words(2, 1)
        for j in range(2):
            error_out(first_bank(j, 1), j, 1)
            quantize_e(j)
        learn_pass(0, 0)
        quantize_u(1, 0)
        learn_pass(0, 1)
        quantize_u(1, 1)
        learn_pass(0, 2)
        learn(1)

        for k in pairs[2:]:
            chores.extend([lambda k=k, c=c: prepare_u(k, c) for c in range(IN_PASSES)])
        for s, span in enumerate(Y_SPANS):
            if span[1] == UNIT:
                chores.extend([lambda s=s, g=g: weigh(s, g, r_rows(g, *Y_SPANS[s])) for g in range(OUT_PASSES)])
        for k in pairs[1:]:
            error(2 * k)
            error(2 * k + 1)
            next_error(k - 1)
            learn(2 * k)
            learn(2 * k + 1)
        for s in range(len(pairs) - 1, len(Y_SPANS)):
            next_error(s)
        for item in list(waiting):
            settle(item[0])
